import numpy as np
import ml_dtypes


def mxq(x, axis, fmt="e4m3"):
    dtype, down = {"e4m3": (ml_dtypes.float8_e4m3fn, 7), "e5m2": (ml_dtypes.float8_e5m2, 14)}[fmt]
    v = np.moveaxis(np.asarray(x, np.float32).astype(ml_dtypes.bfloat16).astype(np.float64), axis, -1)
    blocks = v.reshape(v.shape[:-1] + (-1, 32))
    amax = np.abs(blocks).max(-1, keepdims=True)
    byte = np.maximum(np.where(amax > 0, np.frexp(amax)[1] - 1 + 127, 0) - down, 1)
    scale = np.exp2(byte - 127.0)
    codes = (blocks / scale).astype(np.float32).astype(dtype).astype(np.float64)
    return np.moveaxis((codes * scale).reshape(v.shape), -1, axis)


WIDE = False


def mx_kscale(k):
    if not WIDE:
        return np.ones(k)
    levels = np.array([10, -10, 5, -5, 0])
    if k % 512:
        return np.exp2(np.random.permutation(np.resize(levels, k // 32))).repeat(32)
    a = np.empty((k // 512, 16))
    for p in range(k // 512):
        a[p, :8] = np.random.permutation(np.resize(levels, 8))
        for g in range(8):
            far = levels[np.abs(levels - a[p, g]) >= 10]
            a[p, g + 8] = far[np.random.randint(len(far))]
    return np.exp2(a.ravel()).repeat(32)


def f64(x):
    return np.asarray(x).astype(np.float64)


def striped(idx):
    return np.tile(idx.reshape(-1, 16).T, (8, 1)).astype(np.uint16)


def unstriped(offs):
    return offs[:16].T.reshape(-1).astype(np.int64)


def pack_weight(w):
    k, n = w.shape
    w = f64(np.asarray(w, np.float32).astype(ml_dtypes.bfloat16)).reshape(k // 32, 32, n)
    amax = np.abs(w).max(1)
    byte = np.clip(np.where(amax > 0, np.frexp(amax)[1] - 1 + 127 - 7, 1), 1, 254)
    scaled = (w * np.exp2(127.0 - byte)[:, None, :]).reshape(k, n).astype(np.float32)
    words = np.ascontiguousarray(scaled.reshape(k // 512, 128, 4, n).transpose(0, 1, 3, 2)).astype(ml_dtypes.float8_e4m3fn).view(np.uint8)
    return words, np.ascontiguousarray(byte.astype(np.uint8).reshape(k // 512, 16, n))


def unpack_weight(words, scales):
    g, p, n, _ = words.shape
    vals = np.ascontiguousarray(words).view(ml_dtypes.float8_e4m3fn).astype(np.float64) * np.repeat(np.exp2(scales.astype(np.float64) - 127.0), 8, axis=1)[..., None]
    return vals.transpose(0, 1, 3, 2).reshape(g * 512, n)


K, T, S, H, D, V, W, U = 1024, 2048, 512, 512, 4, 128, 2048, 512


def setup_inputs():
    n = np.random.standard_normal
    s = mx_kscale(K)[:, None]
    u = mx_kscale(H)
    packed_xT = pack_weight(n((K, T)) * s)
    packed_eT = pack_weight(n((H, W)) / np.sqrt(H) / u[:, None])
    return {
        "x_words": packed_xT[0],
        "x_scales": packed_xT[1],
        "w1": (n((K, H)) / np.sqrt(K) / s * u).astype(np.float32),
        "e_words": packed_eT[0],
        "e_scales": packed_eT[1],
        "goal": ((np.random.uniform(size=(S, V)) < 0.01) * 1.0).astype(np.float32),
        "offs": striped(np.random.permutation(T)[:S]),
        "cen": striped(np.random.permutation(W)[:U]),
    }


def reference(x_words, x_scales, w1, e_words, e_scales, goal, offs, cen):
    xq = unpack_weight(x_words, x_scales)[:, unstriped(offs)]
    h = mxq(f64(w1), 0, "e4m3").T @ xq
    e_cen = unpack_weight(e_words, e_scales)[:, unstriped(cen)]
    y = mxq(h, 0, "e4m3").T @ e_cen
    ex = np.exp(2.0 * y)
    es = ex * y
    se = ex.reshape(len(ex), -1, D).sum(axis=2)
    t0 = (es.reshape(len(es), -1, D).sum(axis=2)) / se
    l = 3.0 * (t0 - (0.3 * f64(goal)))
    ex = np.exp(l - l.max(axis=1, keepdims=True))
    return ex / ex.sum(axis=1, keepdims=True)

@@ -1,0 +1,251 @@
+from contextlib import ExitStack
+
+import concourse.mybir as mybir
+from concourse.masks import make_identity
+
+K, T, S, H, D, V, W = 1024, 2048, 512, 512, 4, 128, 2048
+FLOPS = 2 * K * H * S + 2 * H * S * D * V
+
+F32 = mybir.dt.float32
+BF16 = mybir.dt.bfloat16
+I32 = mybir.dt.int32
+U32 = mybir.dt.uint32
+U16 = mybir.dt.uint16
+U8 = mybir.dt.uint8
+FP8X4 = mybir.dt.float8_e4m3fn_x4
+ACT = mybir.ActivationFunctionType
+ALU = mybir.AluOpType
+AX = mybir.AxisListType
+
+P = 128
+PACK = 4
+PASSES = K // (P * PACK)
+CHUNKS = S // P
+HALF = S // 2
+ES_ROW = 8
+WARM = 3
+
+
+def tile_picked_ystrip_soft_p_kernel(
+    tc, x_words, x_scales, w1, e_words, e_scales, goal, offs, cen, out
+):
+    nc = tc.nc
+    with ExitStack() as ctx:
+        keep = ctx.enter_context(tc.tile_pool(name="keep", bufs=1))
+        psum = ctx.enter_context(tc.psum_pool(name="psum", bufs=1))
+
+        def sb(shape, dtype, name, tag=None):
+            return keep.tile(shape, dtype, name=name, tag=tag or name, align_bytes=64)
+
+        def bank(tag, name):
+            return psum.tile([P, PACK, P], F32, name=name, tag=tag)
+
+        offs_sb = sb([P, S // 16], U16, "offs_sb")
+        cen_sb = sb([P, S // 16], U16, "cen_sb")
+        w_raw = [sb([P, PACK, H], F32, f"w_raw{g}") for g in range(PASSES)]
+        x_tab = [sb([P, T], I32, f"x_tab{g}") for g in range(PASSES)]
+        e_tab = sb([P, W], I32, "e_tab")
+        xs_tab = sb([P, T], U8, "xs_tab")
+        es_tab = sb([P, W], U8, "es_tab")
+        goal_sb = sb([P, CHUNKS, V], F32, "goal_sb")
+
+        nc.gpsimd.memset(xs_tab[:].bitcast(I32), 0)
+        nc.gpsimd.memset(es_tab[:].bitcast(I32), 0)
+
+        def load_w(g):
+            rows = w1[g * P * PACK : (g + 1) * P * PACK, :]
+            nc.sync.dma_start(w_raw[g][:], rows.rearrange("(p j) c -> p j c", j=PACK))
+
+        nc.sync.dma_start(offs_sb[:], offs)
+        load_w(0)
+        for q in range(4):
+            nc.sync.dma_start(
+                xs_tab[32 * q : 32 * q + 4 * PASSES, :].bitcast(I32),
+                x_scales[:, 4 * q : 4 * q + 4, :].bitcast(I32),
+            )
+        load_w(1)
+        nc.sync.dma_start(cen_sb[:], cen)
+        for q in range(4):
+            nc.sync.dma_start(
+                es_tab[32 * q + ES_ROW : 32 * q + ES_ROW + 4, :].bitcast(I32),
+                e_scales[0, 4 * q : 4 * q + 4, :].bitcast(I32),
+            )
+        for g in range(PASSES):
+            nc.sync.dma_start(x_tab[g][:], x_words[g].rearrange("p n r -> p (n r)").bitcast(I32))
+        nc.sync.dma_start(e_tab[:], e_words[0].rearrange("p n r -> p (n r)").bitcast(I32))
+        nc.sync.dma_start(goal_sb[:], goal.rearrange("(c p) v -> p c v", p=P))
+
+        ident = sb([P, P], F32, "ident")
+        make_identity(nc, ident[:])
+
+        wq = [sb([P, H], U32, f"wq{g}") for g in range(PASSES)]
+        wq_s = [sb([P, H], U8, "wq_s0")]
+        w_bf = [sb([P, H * PACK], BF16, f"w_bf{g}") for g in range(PASSES)]
+
+        def cast_w(g):
+            nc.scalar.activation(
+                w_bf[g][:].rearrange("p (t m j) -> p m t j", t=PACK, j=PACK),
+                w_raw[g][:].rearrange("p j (m t) -> p m t j", t=PACK),
+                ACT.Copy,
+            )
+
+        def quant_w(g):
+            nc.vector.quantize_mx(wq[g][:].bitcast(FP8X4), wq_s[g][:], w_bf[g][:])
+
+        xs_g = sb([P, S], U8, "xs_g")
+        es_g = sb([P, S], U8, "es_g")
+        es_p = sb([P, S], U8, "es_p")
+        x_g = [[sb([P, HALF], U32, f"x_g{g}_{u}") for u in range(2)] for g in range(PASSES)]
+        e_p = sb([P, S], U32, "e_p")
+
+        cast_w(0)
+        cast_w(1)
+        quant_w(0)
+        nc.vector.tensor_copy(xs_g[:], xs_tab[:].indirect(offs_sb[:]))
+        nc.vector.tensor_copy(es_g[:], es_tab[:].indirect(cen_sb[:]))
+        nc.vector.tensor_copy(
+            es_p[:].rearrange("p (d v) -> p d v", d=D),
+            es_g[:].rearrange("p (v d) -> p d v", d=D),
+        )
+        wq_s.append(sb([P, H], U8, "wq_s1", tag="es_g"))
+        quant_w(1)
+        for g in range(PASSES):
+            for u in range(2):
+                cols = slice(u * HALF // 16, (u + 1) * HALF // 16)
+                nc.vector.tensor_copy(x_g[g][u][:], x_tab[g][:].bitcast(U32).indirect(offs_sb[:, cols]))
+
+        def x_codes(g, c):
+            return x_g[g][c // 2][:, (c % 2) * P : (c % 2 + 1) * P]
+
+        h_bf = [sb([P, P * PACK], BF16, f"h_bf{c}") for c in range(CHUNKS)]
+        hq_first = sb([P, P], U32, "hq_first")
+        hq = [hq_first[:]]
+        hq_s = [sb([P, P], U8, f"hq_s{c}") for c in range(CHUNKS)]
+
+        h_ps = [bank(f"bank{c}", f"h_ps{c}") for c in range(CHUNKS)]
+
+        def h_pass(c, j, g):
+            nc.tensor.matmul_mx(
+                h_ps[c][:, j, :],
+                lhsT=wq[g][:, j * P : (j + 1) * P].bitcast(FP8X4),
+                lhsT_scale=wq_s[g][:, j * P : (j + 1) * P],
+                rhs=x_codes(g, c).bitcast(FP8X4),
+                rhs_scale=xs_g[4 * g : P, c * P : (c + 1) * P],
+                start=(g == 0),
+                stop=(g == PASSES - 1),
+            )
+
+        warm_ps = bank("bank7", "warm_ps")
+
+        def warm_up():
+            nc.tensor.matmul_mx(
+                warm_ps[:, 0:2, :].rearrange("p a b -> p (a b)"),
+                lhsT=wq[0][:, 0:P].bitcast(FP8X4),
+                lhsT_scale=wq_s[0][:, 0:P],
+                rhs=x_g[0][0][:].bitcast(FP8X4),
+                rhs_scale=xs_g[:, 0:HALF],
+                start=True,
+                stop=True,
+            )
+
+        for u in range(2):
+            h_pass(2 * u, 0, 0)
+            h_pass(2 * u + 1, 0, 0)
+            for i in range(WARM):
+                warm_up()
+
+        def project(c):
+            for j in range(PACK):
+                for g in range(PASSES):
+                    if (j, g) != (0, 0):
+                        h_pass(c, j, g)
+            nc.scalar.activation(
+                h_bf[c][:].rearrange("p (t j) -> p t j", j=PACK),
+                h_ps[c][:].rearrange("p j t -> p t j"),
+                ACT.Copy,
+            )
+
+        def quant_h(c):
+            nc.vector.quantize_mx(hq[c].bitcast(FP8X4), hq_s[c][:], h_bf[c][:])
+
+        for c in range(CHUNKS):
+            project(c)
+        quant_h(0)
+        nc.vector.tensor_copy(
+            e_p[:].rearrange("p (d v) -> p v d", d=D),
+            e_tab[:].bitcast(U32).indirect(cen_sb[:]),
+        )
+        hq_rest = sb([P, (CHUNKS - 1) * P], U32, "hq_rest", tag="e_tab")
+        hq.extend(hq_rest[:, i * P : (i + 1) * P] for i in range(CHUNKS - 1))
+        for c in range(1, CHUNKS):
+            quant_h(c)
+
+        ex = [sb([P, D, P], F32, f"ex{c}") for c in range(CHUNKS)]
+        es = [sb([P, D, P], F32, f"es{c}") for c in range(CHUNKS)]
+        y_tags = ["bank4", "bank5", "bank0", "bank1"]
+        for c in range(CHUNKS):
+            y_ps = bank(y_tags[c], f"y_ps{c}")
+            for d in range(D):
+                nc.tensor.matmul_mx(
+                    y_ps[:, d, :],
+                    lhsT=e_p[:, d * V : (d + 1) * V].bitcast(FP8X4),
+                    lhsT_scale=es_p[ES_ROW:P, d * V : (d + 1) * V],
+                    rhs=hq[c].bitcast(FP8X4),
+                    rhs_scale=hq_s[c][:],
+                    start=True,
+                    stop=True,
+                )
+            nc.scalar.activation(ex[c][:], y_ps[:], ACT.Exp, scale=2.0)
+            nc.vector.tensor_tensor(es[c][:], y_ps[:], ex[c][:], ALU.mult)
+
+        sums = [bank(f"bank{6 + u}", f"sums{u}") for u in range(2)]
+
+        def sum_turned(dst, src):
+            for d in range(D):
+                nc.tensor.matmul(
+                    dst, lhsT=src[:, d, :], rhs=ident[:], is_transpose=True, start=(d == 0), stop=(d == D - 1)
+                )
+
+        for c in range(CHUNKS):
+            sum_turned(sums[c // 2][:, c % 2, :], ex[c])
+            if c > 0:
+                sum_turned(sums[(c - 1) // 2][:, 2 + (c - 1) % 2, :], es[c - 1])
+        sum_turned(sums[1][:, 3, :], es[CHUNKS - 1])
+
+        halves = [slice(0, 2), slice(2, 4)]
+        rs = [sb([P, 2, V], F32, f"rs{u}") for u in range(2)]
+        part = [sb([P, 2, V], F32, f"part{u}") for u in range(2)]
+        t3 = [sb([P, 2, V], F32, f"t3_{u}") for u in range(2)]
+        neg = [sb([P, 2, V], F32, f"neg{u}") for u in range(2)]
+        low = [sb([P, 2], F32, f"low{u}") for u in range(2)]
+        prob = [sb([P, 2, V], F32, f"prob{u}") for u in range(2)]
+        tot = [sb([P, 2], F32, f"tot{u}") for u in range(2)]
+        inv = [sb([P, 2], F32, f"inv{u}") for u in range(2)]
+        res = [sb([P, 2, V], F32, f"res{u}") for u in range(2)]
+        for u in range(2):
+            nc.scalar.activation(rs[u][:], sums[u][:, 0:2, :], ACT.Abs_reciprocal_sqrt)
+        for u in range(2):
+            nc.vector.scalar_tensor_tensor(part[u][:], sums[u][:, 2:4, :], 3.0, rs[u][:], ALU.mult, ALU.mult)
+        for u in range(2):
+            nc.vector.tensor_tensor(t3[u][:], part[u][:], rs[u][:], ALU.mult)
+        for u in range(2):
+            nc.vector.scalar_tensor_tensor(
+                neg[u][:], goal_sb[:, halves[u], :], 0.9, t3[u][:], ALU.mult, ALU.subtract
+            )
+        for u in range(2):
+            nc.vector.tensor_reduce(low[u][:], neg[u][:], AX.X, ALU.min)
+        out_v = out.rearrange("(c p) v -> p c v", p=P)
+        for u in range(2):
+            for i in range(2):
+                nc.scalar.activation(
+                    prob[u][:, i, :],
+                    neg[u][:, i, :],
+                    ACT.Exp,
+                    bias=low[u][:, i : i + 1],
+                    scale=-1.0,
+                    accum_out=tot[u][:, i : i + 1],
+                )
+            nc.vector.reciprocal(inv[u][:], tot[u][:])
+            for i in range(2):
+                nc.vector.tensor_scalar(res[u][:, i, :], prob[u][:, i, :], inv[u][:, i : i + 1], None, ALU.mult)
+            nc.sync.dma_start(out_v[:, halves[u], :], res[u][:])

@@ -24,6 +24,7 @@ CHUNKS = S // P
 HALF = S // 2
 ES_ROW = 8
 WARM = 3
+CAST_SPLIT = 96
 
 
 def tile_picked_ystrip_soft_p_kernel(
@@ -49,8 +50,8 @@ def tile_picked_ystrip_soft_p_kernel(
         es_tab = sb([P, W], U8, "es_tab")
         goal_sb = sb([P, CHUNKS, V], F32, "goal_sb")
 
-        nc.gpsimd.memset(xs_tab[:].bitcast(I32), 0)
         nc.gpsimd.memset(es_tab[:].bitcast(I32), 0)
+        nc.vector.memset(xs_tab[:].bitcast(I32), 0)
 
         def load_w(g):
             rows = w1[g * P * PACK : (g + 1) * P * PACK, :]
@@ -60,66 +61,62 @@ def tile_picked_ystrip_soft_p_kernel(
         load_w(0)
         for q in range(4):
             nc.sync.dma_start(
-                xs_tab[32 * q : 32 * q + 4 * PASSES, :].bitcast(I32),
-                x_scales[:, 4 * q : 4 * q + 4, :].bitcast(I32),
-            )
-        load_w(1)
-        nc.sync.dma_start(cen_sb[:], cen)
-        for q in range(4):
-            nc.sync.dma_start(
                 es_tab[32 * q + ES_ROW : 32 * q + ES_ROW + 4, :].bitcast(I32),
                 e_scales[0, 4 * q : 4 * q + 4, :].bitcast(I32),
             )
+        nc.sync.dma_start(cen_sb[:], cen)
+        load_w(1)
         for g in range(PASSES):
             nc.sync.dma_start(x_tab[g][:], x_words[g].rearrange("p n r -> p (n r)").bitcast(I32))
         nc.sync.dma_start(e_tab[:], e_words[0].rearrange("p n r -> p (n r)").bitcast(I32))
         nc.sync.dma_start(goal_sb[:], goal.rearrange("(c p) v -> p c v", p=P))
+        for q in range(4):
+            nc.gpsimd.dma_start(
+                xs_tab[32 * q : 32 * q + 4 * PASSES, :].bitcast(I32),
+                x_scales[:, 4 * q : 4 * q + 4, :].bitcast(I32),
+            )
 
         ident = sb([P, P], F32, "ident")
         make_identity(nc, ident[:])
 
-        wq = [sb([P, H], U32, f"wq{g}") for g in range(PASSES)]
-        wq_s = [sb([P, H], U8, "wq_s0")]
+        wq = [sb([P, H], U32, "wq0")]
+        wq_s = [sb([P, H], U8, f"wq_s{g}") for g in range(PASSES)]
         w_bf = [sb([P, H * PACK], BF16, f"w_bf{g}") for g in range(PASSES)]
 
         def cast_w(g):
-            nc.scalar.activation(
-                w_bf[g][:].rearrange("p (t m j) -> p m t j", t=PACK, j=PACK),
-                w_raw[g][:].rearrange("p j (m t) -> p m t j", t=PACK),
-                ACT.Copy,
-            )
+            dst = w_bf[g][:].rearrange("p (t m j) -> p m t j", t=PACK, j=PACK)
+            src = w_raw[g][:].rearrange("p j (m t) -> p m t j", t=PACK)
+            nc.scalar.activation(dst[:, :CAST_SPLIT], src[:, :CAST_SPLIT], ACT.Copy)
+            nc.vector.tensor_copy(dst[:, CAST_SPLIT:], src[:, CAST_SPLIT:])
 
         def quant_w(g):
             nc.vector.quantize_mx(wq[g][:].bitcast(FP8X4), wq_s[g][:], w_bf[g][:])
 
-        xs_g = sb([P, S], U8, "xs_g")
         es_g = sb([P, S], U8, "es_g")
-        es_p = sb([P, S], U8, "es_p")
         x_g = [[sb([P, HALF], U32, f"x_g{g}_{u}") for u in range(2)] for g in range(PASSES)]
-        e_p = sb([P, S], U32, "e_p")
+        e_g = sb([P, S], U32, "e_g")
 
         cast_w(0)
         cast_w(1)
-        quant_w(0)
-        nc.vector.tensor_copy(xs_g[:], xs_tab[:].indirect(offs_sb[:]))
         nc.vector.tensor_copy(es_g[:], es_tab[:].indirect(cen_sb[:]))
-        nc.vector.tensor_copy(
-            es_p[:].rearrange("p (d v) -> p d v", d=D),
-            es_g[:].rearrange("p (v d) -> p d v", d=D),
-        )
-        wq_s.append(sb([P, H], U8, "wq_s1", tag="es_g"))
-        quant_w(1)
-        for g in range(PASSES):
+        xs_g = sb([P, S], U8, "xs_g", tag="es_tab")
+        nc.vector.tensor_copy(xs_g[:], xs_tab[:].indirect(offs_sb[:]))
+        quant_w(0)
+
+        def gather_x(g):
             for u in range(2):
                 cols = slice(u * HALF // 16, (u + 1) * HALF // 16)
                 nc.vector.tensor_copy(x_g[g][u][:], x_tab[g][:].bitcast(U32).indirect(offs_sb[:, cols]))
+
+        gather_x(0)
+        wq.append(sb([P, H], U32, "wq1", tag="x_tab0"))
+        quant_w(1)
+        gather_x(1)
 
         def x_codes(g, c):
             return x_g[g][c // 2][:, (c % 2) * P : (c % 2 + 1) * P]
 
         h_bf = [sb([P, P * PACK], BF16, f"h_bf{c}") for c in range(CHUNKS)]
-        hq_first = sb([P, P], U32, "hq_first")
-        hq = [hq_first[:]]
         hq_s = [sb([P, P], U8, f"hq_s{c}") for c in range(CHUNKS)]
 
         h_ps = [bank(f"bank{c}", f"h_ps{c}") for c in range(CHUNKS)]
@@ -154,98 +151,104 @@ def tile_picked_ystrip_soft_p_kernel(
             for i in range(WARM):
                 warm_up()
 
+        def h_views(c):
+            return h_bf[c][:].rearrange("p (t j) -> p t j", j=PACK), h_ps[c][:].rearrange("p j t -> p t j")
+
         def project(c):
             for j in range(PACK):
                 for g in range(PASSES):
                     if (j, g) != (0, 0):
                         h_pass(c, j, g)
-            nc.scalar.activation(
-                h_bf[c][:].rearrange("p (t j) -> p t j", j=PACK),
-                h_ps[c][:].rearrange("p j t -> p t j"),
-                ACT.Copy,
-            )
+            if c < CHUNKS - 1:
+                nc.scalar.activation(*h_views(c), ACT.Copy)
 
         def quant_h(c):
             nc.vector.quantize_mx(hq[c].bitcast(FP8X4), hq_s[c][:], h_bf[c][:])
 
         for c in range(CHUNKS):
             project(c)
-        quant_h(0)
-        nc.vector.tensor_copy(
-            e_p[:].rearrange("p (d v) -> p v d", d=D),
-            e_tab[:].bitcast(U32).indirect(cen_sb[:]),
-        )
-        hq_rest = sb([P, (CHUNKS - 1) * P], U32, "hq_rest", tag="e_tab")
-        hq.extend(hq_rest[:, i * P : (i + 1) * P] for i in range(CHUNKS - 1))
-        for c in range(1, CHUNKS):
+        nc.vector.tensor_copy(e_g[:], e_tab[:].bitcast(U32).indirect(cen_sb[:]))
+        hq_all = sb([P, S], U32, "hq_all", tag="e_tab")
+        hq = [hq_all[:, c * P : (c + 1) * P] for c in range(CHUNKS)]
+        for c in range(CHUNKS):
+            if c == CHUNKS - 1:
+                nc.vector.tensor_copy(*h_views(c))
             quant_h(c)
 
-        ex = [sb([P, D, P], F32, f"ex{c}") for c in range(CHUNKS)]
-        es = [sb([P, D, P], F32, f"es{c}") for c in range(CHUNKS)]
+        ex = [sb([P, D, V], F32, f"ex{c}") for c in range(CHUNKS)]
+        es = [sb([P, D, V], F32, f"es{c}") for c in range(CHUNKS)]
         y_tags = ["bank4", "bank5", "bank0", "bank1"]
         for c in range(CHUNKS):
-            y_ps = bank(y_tags[c], f"y_ps{c}")
-            for d in range(D):
-                nc.tensor.matmul_mx(
-                    y_ps[:, d, :],
-                    lhsT=e_p[:, d * V : (d + 1) * V].bitcast(FP8X4),
-                    lhsT_scale=es_p[ES_ROW:P, d * V : (d + 1) * V],
-                    rhs=hq[c].bitcast(FP8X4),
-                    rhs_scale=hq_s[c][:],
-                    start=True,
-                    stop=True,
-                )
-            nc.scalar.activation(ex[c][:], y_ps[:], ACT.Exp, scale=2.0)
-            nc.vector.tensor_tensor(es[c][:], y_ps[:], ex[c][:], ALU.mult)
+            y_ps = psum.tile([P, D * V], F32, name=f"y_ps{c}", tag=y_tags[c])
+            nc.tensor.matmul_mx(
+                y_ps[:],
+                lhsT=hq[c].bitcast(FP8X4),
+                lhsT_scale=hq_s[c][:],
+                rhs=e_g[:].bitcast(FP8X4),
+                rhs_scale=es_g[ES_ROW:P, :],
+                start=True,
+                stop=True,
+            )
+            y_dv = y_ps[:].rearrange("p (v d) -> p d v", d=D)
+            nc.scalar.activation(ex[c][:], y_dv, ACT.Exp, scale=2.0)
+            nc.vector.tensor_tensor(es[c][:], y_dv, ex[c][:], ALU.mult)
 
-        sums = [bank(f"bank{6 + u}", f"sums{u}") for u in range(2)]
+        def turn(dst, src, start, stop):
+            nc.tensor.matmul(dst, lhsT=src, rhs=ident[:], is_transpose=True, start=start, stop=stop)
 
         def sum_turned(dst, src):
-            for d in range(D):
-                nc.tensor.matmul(
-                    dst, lhsT=src[:, d, :], rhs=ident[:], is_transpose=True, start=(d == 0), stop=(d == D - 1)
-                )
+            terms = src.shape[1]
+            for d in range(terms):
+                turn(dst, src[:, d, :], d == 0, d == terms - 1)
 
+        goal_ps = bank("bank2", "goal_ps")
         for c in range(CHUNKS):
-            sum_turned(sums[c // 2][:, c % 2, :], ex[c])
+            turn(goal_ps[:, c, :], goal_sb[:, c, :], True, True)
+
+        sums = [bank(f"bank{6 + u}", f"sums{u}") for u in range(2)]
+        for c in range(CHUNKS):
+            sum_turned(sums[c // 2][:, c % 2, :], ex[c][:])
             if c > 0:
-                sum_turned(sums[(c - 1) // 2][:, 2 + (c - 1) % 2, :], es[c - 1])
-        sum_turned(sums[1][:, 3, :], es[CHUNKS - 1])
+                sum_turned(sums[(c - 1) // 2][:, 2 + (c - 1) % 2, :], es[c - 1][:])
+        sum_turned(sums[1][:, 3, :], es[CHUNKS - 1][:])
+
+        margin = sb([P, CHUNKS, P], F32, "margin")
+        nc.vector.tensor_scalar(margin[:], goal_ps[:], 0.9, None, ALU.mult)
 
         halves = [slice(0, 2), slice(2, 4)]
-        rs = [sb([P, 2, V], F32, f"rs{u}") for u in range(2)]
-        part = [sb([P, 2, V], F32, f"part{u}") for u in range(2)]
-        t3 = [sb([P, 2, V], F32, f"t3_{u}") for u in range(2)]
-        neg = [sb([P, 2, V], F32, f"neg{u}") for u in range(2)]
-        low = [sb([P, 2], F32, f"low{u}") for u in range(2)]
-        prob = [sb([P, 2, V], F32, f"prob{u}") for u in range(2)]
-        tot = [sb([P, 2], F32, f"tot{u}") for u in range(2)]
-        inv = [sb([P, 2], F32, f"inv{u}") for u in range(2)]
+        rs = [sb([P, 2, P], F32, f"rs{u}") for u in range(2)]
+        part = [sb([P, 2, P], F32, f"part{u}") for u in range(2)]
+        t3 = [sb([P, 2, P], F32, f"t3_{u}") for u in range(2)]
+        low = [sb([P, 1], F32, f"low{c}") for c in range(CHUNKS)]
+        prob = [sb([P, V], F32, f"prob{c}") for c in range(CHUNKS)]
+        tot = [sb([P, 1], F32, f"tot{c}") for c in range(CHUNKS)]
+        inv = [sb([P, 1], F32, f"inv{c}") for c in range(CHUNKS)]
         res = [sb([P, 2, V], F32, f"res{u}") for u in range(2)]
+        neg_tags = ["bank3", "bank4", "bank5", "bank0"]
+        neg = [psum.tile([P, V], F32, name=f"neg{c}", tag=neg_tags[c]) for c in range(CHUNKS)]
+        for c in range(CHUNKS):
+            turn(neg[c][:], margin[:, c, :], True, False)
         for u in range(2):
             nc.scalar.activation(rs[u][:], sums[u][:, 0:2, :], ACT.Abs_reciprocal_sqrt)
         for u in range(2):
-            nc.vector.scalar_tensor_tensor(part[u][:], sums[u][:, 2:4, :], 3.0, rs[u][:], ALU.mult, ALU.mult)
+            nc.vector.scalar_tensor_tensor(part[u][:], sums[u][:, 2:4, :], -3.0, rs[u][:], ALU.mult, ALU.mult)
         for u in range(2):
             nc.vector.tensor_tensor(t3[u][:], part[u][:], rs[u][:], ALU.mult)
-        for u in range(2):
-            nc.vector.scalar_tensor_tensor(
-                neg[u][:], goal_sb[:, halves[u], :], 0.9, t3[u][:], ALU.mult, ALU.subtract
-            )
-        for u in range(2):
-            nc.vector.tensor_reduce(low[u][:], neg[u][:], AX.X, ALU.min)
+        for c in range(CHUNKS):
+            turn(neg[c][:], t3[c // 2][:, c % 2, :], False, True)
+            nc.vector.tensor_reduce(low[c][:], neg[c][:], AX.X, ALU.min)
         out_v = out.rearrange("(c p) v -> p c v", p=P)
-        for u in range(2):
-            for i in range(2):
-                nc.scalar.activation(
-                    prob[u][:, i, :],
-                    neg[u][:, i, :],
-                    ACT.Exp,
-                    bias=low[u][:, i : i + 1],
-                    scale=-1.0,
-                    accum_out=tot[u][:, i : i + 1],
-                )
-            nc.vector.reciprocal(inv[u][:], tot[u][:])
-            for i in range(2):
-                nc.vector.tensor_scalar(res[u][:, i, :], prob[u][:, i, :], inv[u][:, i : i + 1], None, ALU.mult)
-            nc.sync.dma_start(out_v[:, halves[u], :], res[u][:])
+        for c in range(CHUNKS):
+            u, i = divmod(c, 2)
+            nc.scalar.activation(
+                prob[c][:],
+                neg[c][:],
+                ACT.Exp,
+                bias=low[c][:],
+                scale=-1.0,
+                accum_out=tot[c][:],
+            )
+            nc.vector.reciprocal(inv[c][:], tot[c][:])
+            nc.vector.tensor_scalar(res[u][:, i, :], prob[c][:], inv[c][:], None, ALU.mult)
+            if i == 1:
+                nc.sync.dma_start(out_v[:, halves[u], :], res[u][:])

@@ -50,8 +50,8 @@ def tile_picked_ystrip_soft_p_kernel(
         es_tab = sb([P, W], U8, "es_tab")
         goal_sb = sb([P, CHUNKS, V], F32, "goal_sb")
 
+        nc.gpsimd.memset(xs_tab[:].bitcast(I32), 0)
         nc.gpsimd.memset(es_tab[:].bitcast(I32), 0)
-        nc.vector.memset(xs_tab[:].bitcast(I32), 0)
 
         def load_w(g):
             rows = w1[g * P * PACK : (g + 1) * P * PACK, :]
@@ -61,20 +61,20 @@ def tile_picked_ystrip_soft_p_kernel(
         load_w(0)
         for q in range(4):
             nc.sync.dma_start(
+                xs_tab[32 * q : 32 * q + 4 * PASSES, :].bitcast(I32),
+                x_scales[:, 4 * q : 4 * q + 4, :].bitcast(I32),
+            )
+        load_w(1)
+        nc.sync.dma_start(cen_sb[:], cen)
+        for q in range(4):
+            nc.sync.dma_start(
                 es_tab[32 * q + ES_ROW : 32 * q + ES_ROW + 4, :].bitcast(I32),
                 e_scales[0, 4 * q : 4 * q + 4, :].bitcast(I32),
             )
-        nc.sync.dma_start(cen_sb[:], cen)
-        load_w(1)
         for g in range(PASSES):
             nc.sync.dma_start(x_tab[g][:], x_words[g].rearrange("p n r -> p (n r)").bitcast(I32))
         nc.sync.dma_start(e_tab[:], e_words[0].rearrange("p n r -> p (n r)").bitcast(I32))
         nc.sync.dma_start(goal_sb[:], goal.rearrange("(c p) v -> p c v", p=P))
-        for q in range(4):
-            nc.gpsimd.dma_start(
-                xs_tab[32 * q : 32 * q + 4 * PASSES, :].bitcast(I32),
-                x_scales[:, 4 * q : 4 * q + 4, :].bitcast(I32),
-            )
 
         ident = sb([P, P], F32, "ident")
         make_identity(nc, ident[:])
@@ -92,16 +92,16 @@ def tile_picked_ystrip_soft_p_kernel(
         def quant_w(g):
             nc.vector.quantize_mx(wq[g][:].bitcast(FP8X4), wq_s[g][:], w_bf[g][:])
 
+        xs_g = sb([P, S], U8, "xs_g")
         es_g = sb([P, S], U8, "es_g")
         x_g = [[sb([P, HALF], U32, f"x_g{g}_{u}") for u in range(2)] for g in range(PASSES)]
         e_g = sb([P, S], U32, "e_g")
 
         cast_w(0)
         cast_w(1)
-        nc.vector.tensor_copy(es_g[:], es_tab[:].indirect(cen_sb[:]))
-        xs_g = sb([P, S], U8, "xs_g", tag="es_tab")
         nc.vector.tensor_copy(xs_g[:], xs_tab[:].indirect(offs_sb[:]))
         quant_w(0)
+        nc.vector.tensor_copy(es_g[:], es_tab[:].indirect(cen_sb[:]))
 
         def gather_x(g):
             for u in range(2):

@@ -57,13 +57,13 @@ def tile_picked_ystrip_soft_p_kernel(
             rows = w1[g * P * PACK : (g + 1) * P * PACK, :]
             nc.sync.dma_start(w_raw[g][:], rows.rearrange("(p j) c -> p j c", j=PACK))
 
-        nc.sync.dma_start(offs_sb[:], offs)
-        load_w(0)
         for q in range(4):
             nc.sync.dma_start(
                 xs_tab[32 * q : 32 * q + 4 * PASSES, :].bitcast(I32),
                 x_scales[:, 4 * q : 4 * q + 4, :].bitcast(I32),
             )
+        nc.sync.dma_start(offs_sb[:], offs)
+        load_w(0)
         load_w(1)
         nc.sync.dma_start(cen_sb[:], cen)
         for q in range(4):
@@ -94,7 +94,6 @@ def tile_picked_ystrip_soft_p_kernel(
 
         xs_g = sb([P, S], U8, "xs_g")
         es_g = sb([P, S], U8, "es_g")
-        x_g = [[sb([P, HALF], U32, f"x_g{g}_{u}") for u in range(2)] for g in range(PASSES)]
         e_g = sb([P, S], U32, "e_g")
 
         cast_w(0)
@@ -102,6 +101,10 @@ def tile_picked_ystrip_soft_p_kernel(
         nc.vector.tensor_copy(xs_g[:], xs_tab[:].indirect(offs_sb[:]))
         quant_w(0)
         nc.vector.tensor_copy(es_g[:], es_tab[:].indirect(cen_sb[:]))
+        x_g = [
+            [sb([P, HALF], U32, f"x_g{g}_{u}", tag="es_tab" if (g, u) == (0, 0) else None) for u in range(2)]
+            for g in range(PASSES)
+        ]
 
         def gather_x(g):
             for u in range(2):
@@ -116,7 +119,7 @@ def tile_picked_ystrip_soft_p_kernel(
         def x_codes(g, c):
             return x_g[g][c // 2][:, (c % 2) * P : (c % 2 + 1) * P]
 
-        h_bf = [sb([P, P * PACK], BF16, f"h_bf{c}") for c in range(CHUNKS)]
+        h_bf = [sb([P, P * PACK], BF16, f"h_bf{c}") for c in range(CHUNKS - 1)]
         hq_s = [sb([P, P], U8, f"hq_s{c}") for c in range(CHUNKS)]
 
         h_ps = [bank(f"bank{c}", f"h_ps{c}") for c in range(CHUNKS)]
@@ -172,11 +175,13 @@ def tile_picked_ystrip_soft_p_kernel(
         hq = [hq_all[:, c * P : (c + 1) * P] for c in range(CHUNKS)]
         for c in range(CHUNKS):
             if c == CHUNKS - 1:
+                h_bf.append(sb([P, P * PACK], BF16, "h_bf_last", tag=f"h_bf{c - 1}"))
                 nc.vector.tensor_copy(*h_views(c))
             quant_h(c)
 
         ex = [sb([P, D, V], F32, f"ex{c}") for c in range(CHUNKS)]
-        es = [sb([P, D, V], F32, f"es{c}") for c in range(CHUNKS)]
+        es = [sb([P, D, V], F32, f"es{c}", tag=f"h_bf{CHUNKS - 2}" if c == 0 else None) for c in range(CHUNKS)]
+        ex2 = [sb([P, 2, V], F32, f"ex2_{c}") for c in range(CHUNKS - 1)]
         y_tags = ["bank4", "bank5", "bank0", "bank1"]
         for c in range(CHUNKS):
             y_ps = psum.tile([P, D * V], F32, name=f"y_ps{c}", tag=y_tags[c])
@@ -192,6 +197,8 @@ def tile_picked_ystrip_soft_p_kernel(
             y_dv = y_ps[:].rearrange("p (v d) -> p d v", d=D)
             nc.scalar.activation(ex[c][:], y_dv, ACT.Exp, scale=2.0)
             nc.vector.tensor_tensor(es[c][:], y_dv, ex[c][:], ALU.mult)
+            if c < CHUNKS - 1:
+                nc.gpsimd.tensor_tensor(ex2[c][:], ex[c][:, 0:2, :], ex[c][:, 2:4, :], ALU.add)
 
         def turn(dst, src, start, stop):
             nc.tensor.matmul(dst, lhsT=src, rhs=ident[:], is_transpose=True, start=start, stop=stop)
@@ -201,18 +208,18 @@ def tile_picked_ystrip_soft_p_kernel(
             for d in range(terms):
                 turn(dst, src[:, d, :], d == 0, d == terms - 1)
 
-        goal_ps = bank("bank2", "goal_ps")
+        goal_ps = bank("bank3", "goal_ps")
         for c in range(CHUNKS):
             turn(goal_ps[:, c, :], goal_sb[:, c, :], True, True)
 
         sums = [bank(f"bank{6 + u}", f"sums{u}") for u in range(2)]
         for c in range(CHUNKS):
-            sum_turned(sums[c // 2][:, c % 2, :], ex[c][:])
+            sum_turned(sums[c // 2][:, c % 2, :], ex2[c][:] if c < CHUNKS - 1 else ex[c][:])
             if c > 0:
                 sum_turned(sums[(c - 1) // 2][:, 2 + (c - 1) % 2, :], es[c - 1][:])
         sum_turned(sums[1][:, 3, :], es[CHUNKS - 1][:])
 
-        margin = sb([P, CHUNKS, P], F32, "margin")
+        margin = sb([P, CHUNKS, P], F32, "margin", tag=f"ex{CHUNKS - 1}")
         nc.vector.tensor_scalar(margin[:], goal_ps[:], 0.9, None, ALU.mult)
 
         halves = [slice(0, 2), slice(2, 4)]
@@ -221,10 +228,10 @@ def tile_picked_ystrip_soft_p_kernel(
         t3 = [sb([P, 2, P], F32, f"t3_{u}") for u in range(2)]
         low = [sb([P, 1], F32, f"low{c}") for c in range(CHUNKS)]
         prob = [sb([P, V], F32, f"prob{c}") for c in range(CHUNKS)]
-        tot = [sb([P, 1], F32, f"tot{c}") for c in range(CHUNKS)]
-        inv = [sb([P, 1], F32, f"inv{c}") for c in range(CHUNKS)]
+        tot = [sb([P, 2], F32, f"tot{u}") for u in range(2)]
+        inv = [sb([P, 2], F32, f"inv{u}") for u in range(2)]
         res = [sb([P, 2, V], F32, f"res{u}") for u in range(2)]
-        neg_tags = ["bank3", "bank4", "bank5", "bank0"]
+        neg_tags = ["bank2", "bank4", "bank5", "bank0"]
         neg = [psum.tile([P, V], F32, name=f"neg{c}", tag=neg_tags[c]) for c in range(CHUNKS)]
         for c in range(CHUNKS):
             turn(neg[c][:], margin[:, c, :], True, False)
@@ -246,9 +253,10 @@ def tile_picked_ystrip_soft_p_kernel(
                 ACT.Exp,
                 bias=low[c][:],
                 scale=-1.0,
-                accum_out=tot[c][:],
+                accum_out=tot[u][:, i : i + 1],
             )
-            nc.vector.reciprocal(inv[c][:], tot[c][:])
-            nc.vector.tensor_scalar(res[u][:, i, :], prob[c][:], inv[c][:], None, ALU.mult)
             if i == 1:
+                nc.vector.reciprocal(inv[u][:], tot[u][:])
+                for k in range(2):
+                    nc.vector.tensor_scalar(res[u][:, k, :], prob[2 * u + k][:], inv[u][:, k : k + 1], None, ALU.mult)
                 nc.sync.dma_start(out_v[:, halves[u], :], res[u][:])

@@ -181,7 +181,6 @@ def tile_picked_ystrip_soft_p_kernel(
 
         ex = [sb([P, D, V], F32, f"ex{c}") for c in range(CHUNKS)]
         es = [sb([P, D, V], F32, f"es{c}", tag=f"h_bf{CHUNKS - 2}" if c == 0 else None) for c in range(CHUNKS)]
-        ex2 = [sb([P, 2, V], F32, f"ex2_{c}") for c in range(CHUNKS - 1)]
         y_tags = ["bank4", "bank5", "bank0", "bank1"]
         for c in range(CHUNKS):
             y_ps = psum.tile([P, D * V], F32, name=f"y_ps{c}", tag=y_tags[c])
@@ -197,8 +196,6 @@ def tile_picked_ystrip_soft_p_kernel(
             y_dv = y_ps[:].rearrange("p (v d) -> p d v", d=D)
             nc.scalar.activation(ex[c][:], y_dv, ACT.Exp, scale=2.0)
             nc.vector.tensor_tensor(es[c][:], y_dv, ex[c][:], ALU.mult)
-            if c < CHUNKS - 1:
-                nc.gpsimd.tensor_tensor(ex2[c][:], ex[c][:, 0:2, :], ex[c][:, 2:4, :], ALU.add)
 
         def turn(dst, src, start, stop):
             nc.tensor.matmul(dst, lhsT=src, rhs=ident[:], is_transpose=True, start=start, stop=stop)
@@ -212,12 +209,14 @@ def tile_picked_ystrip_soft_p_kernel(
         for c in range(CHUNKS):
             turn(goal_ps[:, c, :], goal_sb[:, c, :], True, True)
 
-        sums = [bank(f"bank{6 + u}", f"sums{u}") for u in range(2)]
+        se_ps = bank("bank6", "se_ps")
+        ses_tags = ["bank7", "bank2"]
+        ses_ps = [psum.tile([P, 2, P], F32, name=f"ses_ps{u}", tag=ses_tags[u]) for u in range(2)]
         for c in range(CHUNKS):
-            sum_turned(sums[c // 2][:, c % 2, :], ex2[c][:] if c < CHUNKS - 1 else ex[c][:])
+            sum_turned(se_ps[:, c, :], ex[c][:])
             if c > 0:
-                sum_turned(sums[(c - 1) // 2][:, 2 + (c - 1) % 2, :], es[c - 1][:])
-        sum_turned(sums[1][:, 3, :], es[CHUNKS - 1][:])
+                sum_turned(ses_ps[(c - 1) // 2][:, (c - 1) % 2, :], es[c - 1][:])
+        sum_turned(ses_ps[1][:, 1, :], es[CHUNKS - 1][:])
 
         margin = sb([P, CHUNKS, P], F32, "margin", tag=f"ex{CHUNKS - 1}")
         nc.vector.tensor_scalar(margin[:], goal_ps[:], 0.9, None, ALU.mult)
@@ -231,14 +230,14 @@ def tile_picked_ystrip_soft_p_kernel(
         tot = [sb([P, 2], F32, f"tot{u}") for u in range(2)]
         inv = [sb([P, 2], F32, f"inv{u}") for u in range(2)]
         res = [sb([P, 2, V], F32, f"res{u}") for u in range(2)]
-        neg_tags = ["bank2", "bank4", "bank5", "bank0"]
+        neg_tags = ["bank3", "bank4", "bank5", "bank0"]
         neg = [psum.tile([P, V], F32, name=f"neg{c}", tag=neg_tags[c]) for c in range(CHUNKS)]
         for c in range(CHUNKS):
             turn(neg[c][:], margin[:, c, :], True, False)
         for u in range(2):
-            nc.scalar.activation(rs[u][:], sums[u][:, 0:2, :], ACT.Abs_reciprocal_sqrt)
+            nc.scalar.activation(rs[u][:], se_ps[:, halves[u], :], ACT.Abs_reciprocal_sqrt)
         for u in range(2):
-            nc.vector.scalar_tensor_tensor(part[u][:], sums[u][:, 2:4, :], -3.0, rs[u][:], ALU.mult, ALU.mult)
+            nc.vector.scalar_tensor_tensor(part[u][:], ses_ps[u][:], -3.0, rs[u][:], ALU.mult, ALU.mult)
         for u in range(2):
             nc.vector.tensor_tensor(t3[u][:], part[u][:], rs[u][:], ALU.mult)
         for c in range(CHUNKS):

@@ -23,7 +23,6 @@ PASSES = K // (P * PACK)
 CHUNKS = S // P
 HALF = S // 2
 ES_ROW = 8
-WARM = 3
 CAST_SPLIT = 96
 
 
@@ -135,24 +134,9 @@ def tile_picked_ystrip_soft_p_kernel(
                 stop=(g == PASSES - 1),
             )
 
-        warm_ps = bank("bank7", "warm_ps")
-
-        def warm_up():
-            nc.tensor.matmul_mx(
-                warm_ps[:, 0:2, :].rearrange("p a b -> p (a b)"),
-                lhsT=wq[0][:, 0:P].bitcast(FP8X4),
-                lhsT_scale=wq_s[0][:, 0:P],
-                rhs=x_g[0][0][:].bitcast(FP8X4),
-                rhs_scale=xs_g[:, 0:HALF],
-                start=True,
-                stop=True,
-            )
-
         for u in range(2):
             h_pass(2 * u, 0, 0)
             h_pass(2 * u + 1, 0, 0)
-            for i in range(WARM):
-                warm_up()
 
         def h_views(c):
             return h_bf[c][:].rearrange("p (t j) -> p t j", j=PACK), h_ps[c][:].rearrange("p j t -> p t j")

@@ -23,7 +23,7 @@ PASSES = K // (P * PACK)
 CHUNKS = S // P
 HALF = S // 2
 ES_ROW = 8
-CAST_SPLIT = 96
+CAST_SPLIT = 64
 
 
 def tile_picked_ystrip_soft_p_kernel(
@@ -37,8 +37,8 @@ def tile_picked_ystrip_soft_p_kernel(
         def sb(shape, dtype, name, tag=None):
             return keep.tile(shape, dtype, name=name, tag=tag or name, align_bytes=64)
 
-        def bank(tag, name):
-            return psum.tile([P, PACK, P], F32, name=name, tag=tag)
+        def bank(n, name):
+            return psum.tile([P, PACK, P], F32, name=name, tag=f"bank{n}")
 
         offs_sb = sb([P, S // 16], U16, "offs_sb")
         cen_sb = sb([P, S // 16], U16, "cen_sb")
@@ -56,6 +56,9 @@ def tile_picked_ystrip_soft_p_kernel(
             rows = w1[g * P * PACK : (g + 1) * P * PACK, :]
             nc.sync.dma_start(w_raw[g][:], rows.rearrange("(p j) c -> p j c", j=PACK))
 
+        def load_x(g):
+            nc.sync.dma_start(x_tab[g][:], x_words[g].rearrange("p n r -> p (n r)").bitcast(I32))
+
         for q in range(4):
             nc.sync.dma_start(
                 xs_tab[32 * q : 32 * q + 4 * PASSES, :].bitcast(I32),
@@ -64,21 +67,21 @@ def tile_picked_ystrip_soft_p_kernel(
         nc.sync.dma_start(offs_sb[:], offs)
         load_w(0)
         load_w(1)
+        load_x(0)
         nc.sync.dma_start(cen_sb[:], cen)
+        load_x(1)
         for q in range(4):
             nc.sync.dma_start(
                 es_tab[32 * q + ES_ROW : 32 * q + ES_ROW + 4, :].bitcast(I32),
                 e_scales[0, 4 * q : 4 * q + 4, :].bitcast(I32),
             )
-        for g in range(PASSES):
-            nc.sync.dma_start(x_tab[g][:], x_words[g].rearrange("p n r -> p (n r)").bitcast(I32))
         nc.sync.dma_start(e_tab[:], e_words[0].rearrange("p n r -> p (n r)").bitcast(I32))
         nc.sync.dma_start(goal_sb[:], goal.rearrange("(c p) v -> p c v", p=P))
 
         ident = sb([P, P], F32, "ident")
         make_identity(nc, ident[:])
 
-        wq = [sb([P, H], U32, "wq0")]
+        wq = [sb([P, H], U32, f"wq{g}") for g in range(PASSES)]
         wq_s = [sb([P, H], U8, f"wq_s{g}") for g in range(PASSES)]
         w_bf = [sb([P, H * PACK], BF16, f"w_bf{g}") for g in range(PASSES)]
 
@@ -92,154 +95,135 @@ def tile_picked_ystrip_soft_p_kernel(
             nc.vector.quantize_mx(wq[g][:].bitcast(FP8X4), wq_s[g][:], w_bf[g][:])
 
         xs_g = sb([P, S], U8, "xs_g")
-        es_g = sb([P, S], U8, "es_g")
         e_g = sb([P, S], U32, "e_g")
-
-        cast_w(0)
-        cast_w(1)
-        nc.vector.tensor_copy(xs_g[:], xs_tab[:].indirect(offs_sb[:]))
-        quant_w(0)
-        nc.vector.tensor_copy(es_g[:], es_tab[:].indirect(cen_sb[:]))
-        x_g = [
-            [sb([P, HALF], U32, f"x_g{g}_{u}", tag="es_tab" if (g, u) == (0, 0) else None) for u in range(2)]
-            for g in range(PASSES)
-        ]
+        x_g = [[sb([P, HALF], U32, f"x_g{g}_{u}") for u in range(2)] for g in range(PASSES)]
 
         def gather_x(g):
             for u in range(2):
                 cols = slice(u * HALF // 16, (u + 1) * HALF // 16)
                 nc.vector.tensor_copy(x_g[g][u][:], x_tab[g][:].bitcast(U32).indirect(offs_sb[:, cols]))
 
-        gather_x(0)
-        wq.append(sb([P, H], U32, "wq1", tag="x_tab0"))
+        nc.vector.tensor_copy(xs_g[:], xs_tab[:].indirect(offs_sb[:]))
+        cast_w(0)
+        quant_w(0)
+        cast_w(1)
         quant_w(1)
+        gather_x(0)
         gather_x(1)
+        es_g = sb([P, S], U8, "es_g")
+        nc.vector.tensor_copy(es_g[:], es_tab[:].indirect(cen_sb[:]))
 
-        def x_codes(g, c):
-            return x_g[g][c // 2][:, (c % 2) * P : (c % 2 + 1) * P]
+        h_ps = [bank(c, f"h_ps{c}") for c in range(CHUNKS)]
+        for g in range(PASSES):
+            for c in range(CHUNKS):
+                for j in range(PACK):
+                    nc.tensor.matmul_mx(
+                        h_ps[c][:, j, :],
+                        lhsT=wq[g][:, j * P : (j + 1) * P].bitcast(FP8X4),
+                        lhsT_scale=wq_s[g][:, j * P : (j + 1) * P],
+                        rhs=x_g[g][c // 2][:, (c % 2) * P : (c % 2 + 1) * P].bitcast(FP8X4),
+                        rhs_scale=xs_g[4 * g : P, c * P : (c + 1) * P],
+                        start=(g == 0 and j == 0),
+                        stop=(g == PASSES - 1 and j == PACK - 1),
+                    )
 
-        h_bf = [sb([P, P * PACK], BF16, f"h_bf{c}") for c in range(CHUNKS - 1)]
+        h_bf = [sb([P, P * PACK], BF16, f"h_bf{c}") for c in range(CHUNKS)]
         hq_s = [sb([P, P], U8, f"hq_s{c}") for c in range(CHUNKS)]
+        for c in range(CHUNKS):
+            dst = h_bf[c][:].rearrange("p (t j) -> p t j", j=PACK)
+            src = h_ps[c][:].rearrange("p j t -> p t j")
+            nc.scalar.activation(dst, src, ACT.Copy)
 
-        h_ps = [bank(f"bank{c}", f"h_ps{c}") for c in range(CHUNKS)]
+        def quant_h(c, codes):
+            nc.vector.quantize_mx(codes.bitcast(FP8X4), hq_s[c][:], h_bf[c][:])
 
-        def h_pass(c, j, g):
-            nc.tensor.matmul_mx(
-                h_ps[c][:, j, :],
-                lhsT=wq[g][:, j * P : (j + 1) * P].bitcast(FP8X4),
-                lhsT_scale=wq_s[g][:, j * P : (j + 1) * P],
-                rhs=x_codes(g, c).bitcast(FP8X4),
-                rhs_scale=xs_g[4 * g : P, c * P : (c + 1) * P],
-                start=(g == 0),
-                stop=(g == PASSES - 1),
-            )
-
+        hq_early = sb([P, HALF], U32, "hq_early", tag="es_tab")
+        hq = [hq_early[:, c * P : (c + 1) * P] for c in range(2)]
+        for c in range(2):
+            quant_h(c, hq[c])
         for u in range(2):
-            h_pass(2 * u, 0, 0)
-            h_pass(2 * u + 1, 0, 0)
-
-        def h_views(c):
-            return h_bf[c][:].rearrange("p (t j) -> p t j", j=PACK), h_ps[c][:].rearrange("p j t -> p t j")
-
-        def project(c):
-            for j in range(PACK):
-                for g in range(PASSES):
-                    if (j, g) != (0, 0):
-                        h_pass(c, j, g)
-            if c < CHUNKS - 1:
-                nc.scalar.activation(*h_views(c), ACT.Copy)
-
-        def quant_h(c):
-            nc.vector.quantize_mx(hq[c].bitcast(FP8X4), hq_s[c][:], h_bf[c][:])
-
-        for c in range(CHUNKS):
-            project(c)
-        nc.vector.tensor_copy(e_g[:], e_tab[:].bitcast(U32).indirect(cen_sb[:]))
-        hq_all = sb([P, S], U32, "hq_all", tag="e_tab")
-        hq = [hq_all[:, c * P : (c + 1) * P] for c in range(CHUNKS)]
-        for c in range(CHUNKS):
-            if c == CHUNKS - 1:
-                h_bf.append(sb([P, P * PACK], BF16, "h_bf_last", tag=f"h_bf{c - 1}"))
-                nc.vector.tensor_copy(*h_views(c))
-            quant_h(c)
-
-        ex = [sb([P, D, V], F32, f"ex{c}") for c in range(CHUNKS)]
-        es = [sb([P, D, V], F32, f"es{c}", tag=f"h_bf{CHUNKS - 2}" if c == 0 else None) for c in range(CHUNKS)]
-        y_tags = ["bank4", "bank5", "bank0", "bank1"]
-        for c in range(CHUNKS):
-            y_ps = psum.tile([P, D * V], F32, name=f"y_ps{c}", tag=y_tags[c])
-            nc.tensor.matmul_mx(
-                y_ps[:],
-                lhsT=hq[c].bitcast(FP8X4),
-                lhsT_scale=hq_s[c][:],
-                rhs=e_g[:].bitcast(FP8X4),
-                rhs_scale=es_g[ES_ROW:P, :],
-                start=True,
-                stop=True,
-            )
-            y_dv = y_ps[:].rearrange("p (v d) -> p d v", d=D)
-            nc.scalar.activation(ex[c][:], y_dv, ACT.Exp, scale=2.0)
-            nc.vector.tensor_tensor(es[c][:], y_dv, ex[c][:], ALU.mult)
+            cols = slice(u * HALF // 16, (u + 1) * HALF // 16)
+            nc.vector.tensor_copy(e_g[:, u * HALF : (u + 1) * HALF], e_tab[:].bitcast(U32).indirect(cen_sb[:, cols]))
+        hq_late = sb([P, HALF], U32, "hq_late", tag="e_tab")
+        hq.extend(hq_late[:, c * P : (c + 1) * P] for c in range(2))
+        for c in range(2, CHUNKS):
+            quant_h(c, hq[c])
 
         def turn(dst, src, start, stop):
             nc.tensor.matmul(dst, lhsT=src, rhs=ident[:], is_transpose=True, start=start, stop=stop)
 
         def sum_turned(dst, src):
-            terms = src.shape[1]
-            for d in range(terms):
-                turn(dst, src[:, d, :], d == 0, d == terms - 1)
+            for d in range(D):
+                turn(dst, src[:, d, :], d == 0, d == D - 1)
 
-        goal_ps = bank("bank3", "goal_ps")
+        ex = [sb([P, D, V], F32, f"ex{c}") for c in range(CHUNKS)]
+        es = [sb([P, D, V], F32, f"es{c}") for c in range(CHUNKS)]
+
+        def similarity(c, n, first, width):
+            y_ps = psum.tile([P, width], F32, name=f"y_ps{c}_{first}", tag=f"bank{n}")
+            nc.tensor.matmul_mx(
+                y_ps[:],
+                lhsT=hq[c].bitcast(FP8X4),
+                lhsT_scale=hq_s[c][:],
+                rhs=e_g[:, first : first + width].bitcast(FP8X4),
+                rhs_scale=es_g[ES_ROW:P, first : first + width],
+                start=True,
+                stop=True,
+            )
+            y_dv = y_ps[:].rearrange("p (v d) -> p d v", d=D)
+            classes = slice(first // D, (first + width) // D)
+            nc.scalar.activation(ex[c][:, :, classes], y_dv, ACT.Exp, scale=2.0)
+            nc.vector.tensor_tensor(es[c][:, :, classes], y_dv, ex[c][:, :, classes], ALU.mult)
+
+        for c in range(2):
+            similarity(c, 4 + c, 0, HALF)
+        for c in range(2):
+            similarity(c, 1 + c, HALF, HALF)
+        for c in range(2, CHUNKS):
+            similarity(c, 4 + c, 0, S)
+
+        goal_ps = bank(3, "goal_ps")
         for c in range(CHUNKS):
             turn(goal_ps[:, c, :], goal_sb[:, c, :], True, True)
+        margin = sb([P, CHUNKS, P], F32, "margin")
+        nc.vector.tensor_scalar(margin[:], goal_ps[:], 0.9, None, ALU.mult)
 
-        se_ps = bank("bank6", "se_ps")
-        ses_tags = ["bank7", "bank2"]
-        ses_ps = [psum.tile([P, 2, P], F32, name=f"ses_ps{u}", tag=ses_tags[u]) for u in range(2)]
+        se_ps = bank(0, "se_ps")
+        ses_ps = [psum.tile([P, 2, P], F32, name=f"ses_ps{u}", tag=f"bank{1 + u}") for u in range(2)]
         for c in range(CHUNKS):
             sum_turned(se_ps[:, c, :], ex[c][:])
             if c > 0:
                 sum_turned(ses_ps[(c - 1) // 2][:, (c - 1) % 2, :], es[c - 1][:])
         sum_turned(ses_ps[1][:, 1, :], es[CHUNKS - 1][:])
 
-        margin = sb([P, CHUNKS, P], F32, "margin", tag=f"ex{CHUNKS - 1}")
-        nc.vector.tensor_scalar(margin[:], goal_ps[:], 0.9, None, ALU.mult)
-
-        halves = [slice(0, 2), slice(2, 4)]
-        rs = [sb([P, 2, P], F32, f"rs{u}") for u in range(2)]
-        part = [sb([P, 2, P], F32, f"part{u}") for u in range(2)]
-        t3 = [sb([P, 2, P], F32, f"t3_{u}") for u in range(2)]
+        rs = [sb([P, P], F32, f"rs{c}") for c in range(CHUNKS)]
+        part = [sb([P, P], F32, f"part{c}") for c in range(CHUNKS)]
+        t3 = [sb([P, P], F32, f"t3_{c}") for c in range(CHUNKS)]
         low = [sb([P, 1], F32, f"low{c}") for c in range(CHUNKS)]
         prob = [sb([P, V], F32, f"prob{c}") for c in range(CHUNKS)]
-        tot = [sb([P, 2], F32, f"tot{u}") for u in range(2)]
-        inv = [sb([P, 2], F32, f"inv{u}") for u in range(2)]
-        res = [sb([P, 2, V], F32, f"res{u}") for u in range(2)]
-        neg_tags = ["bank3", "bank4", "bank5", "bank0"]
-        neg = [psum.tile([P, V], F32, name=f"neg{c}", tag=neg_tags[c]) for c in range(CHUNKS)]
+        tot = [sb([P, 1], F32, f"tot{c}") for c in range(CHUNKS)]
+        inv = [sb([P, 1], F32, f"inv{c}") for c in range(CHUNKS)]
+        res = [sb([P, V], F32, f"res{c}") for c in range(CHUNKS)]
+        neg = [psum.tile([P, V], F32, name=f"neg{c}", tag=f"bank{4 + c}") for c in range(CHUNKS)]
         for c in range(CHUNKS):
             turn(neg[c][:], margin[:, c, :], True, False)
-        for u in range(2):
-            nc.scalar.activation(rs[u][:], se_ps[:, halves[u], :], ACT.Abs_reciprocal_sqrt)
-        for u in range(2):
-            nc.vector.scalar_tensor_tensor(part[u][:], ses_ps[u][:], -3.0, rs[u][:], ALU.mult, ALU.mult)
-        for u in range(2):
-            nc.vector.tensor_tensor(t3[u][:], part[u][:], rs[u][:], ALU.mult)
         for c in range(CHUNKS):
-            turn(neg[c][:], t3[c // 2][:, c % 2, :], False, True)
+            nc.scalar.activation(rs[c][:], se_ps[:, c, :], ACT.Abs_reciprocal_sqrt)
+        for c in range(CHUNKS + 1):
+            if c < CHUNKS:
+                nc.vector.scalar_tensor_tensor(
+                    part[c][:], ses_ps[c // 2][:, c % 2, :], -3.0, rs[c][:], ALU.mult, ALU.mult
+                )
+            if c > 0:
+                nc.vector.tensor_tensor(t3[c - 1][:], part[c - 1][:], rs[c - 1][:], ALU.mult)
+        for c in range(CHUNKS):
+            turn(neg[c][:], t3[c][:], False, True)
             nc.vector.tensor_reduce(low[c][:], neg[c][:], AX.X, ALU.min)
-        out_v = out.rearrange("(c p) v -> p c v", p=P)
         for c in range(CHUNKS):
-            u, i = divmod(c, 2)
-            nc.scalar.activation(
-                prob[c][:],
-                neg[c][:],
-                ACT.Exp,
-                bias=low[c][:],
-                scale=-1.0,
-                accum_out=tot[u][:, i : i + 1],
-            )
-            if i == 1:
-                nc.vector.reciprocal(inv[u][:], tot[u][:])
-                for k in range(2):
-                    nc.vector.tensor_scalar(res[u][:, k, :], prob[2 * u + k][:], inv[u][:, k : k + 1], None, ALU.mult)
-                nc.sync.dma_start(out_v[:, halves[u], :], res[u][:])
+            nc.scalar.activation(prob[c][:], neg[c][:], ACT.Exp, bias=low[c][:], scale=-1.0, accum_out=tot[c][:])
+        for c in range(CHUNKS + 1):
+            if c < CHUNKS:
+                nc.vector.reciprocal(inv[c][:], tot[c][:])
+            if c > 0:
+                nc.vector.tensor_scalar(res[c - 1][:], prob[c - 1][:], inv[c - 1][:], None, ALU.mult)
+                nc.sync.dma_start(out[(c - 1) * P : c * P, :], res[c - 1][:])

@@ -43,40 +43,38 @@ def tile_picked_ystrip_soft_p_kernel(
         offs_sb = sb([P, S // 16], U16, "offs_sb")
         cen_sb = sb([P, S // 16], U16, "cen_sb")
         w_raw = [sb([P, PACK, H], F32, f"w_raw{g}") for g in range(PASSES)]
-        x_tab = [sb([P, T], I32, f"x_tab{g}") for g in range(PASSES)]
-        e_tab = sb([P, W], I32, "e_tab")
         xs_tab = sb([P, T], U8, "xs_tab")
         es_tab = sb([P, W], U8, "es_tab")
-        goal_sb = sb([P, CHUNKS, V], F32, "goal_sb")
+        xs_c = sb([P, S], U8, "xs_c")
+        es_c = sb([P, S], U8, "es_c")
+        xs_g = [sb([P, S], U8, f"xs_g{g}") for g in range(PASSES)]
+        es_g = sb([P, S], U8, "es_g")
 
-        nc.gpsimd.memset(xs_tab[:].bitcast(I32), 0)
-        nc.gpsimd.memset(es_tab[:].bitcast(I32), 0)
+        for plane in (xs_tab, es_tab, *xs_g, es_g):
+            nc.gpsimd.memset(plane[:].bitcast(I32), 0)
 
         def load_w(g):
             rows = w1[g * P * PACK : (g + 1) * P * PACK, :]
             nc.sync.dma_start(w_raw[g][:], rows.rearrange("(p j) c -> p j c", j=PACK))
 
-        def load_x(g):
-            nc.sync.dma_start(x_tab[g][:], x_words[g].rearrange("p n r -> p (n r)").bitcast(I32))
+        def load_words(tab, words):
+            nc.sync.dma_start(tab[:], words.rearrange("p n r -> p (n r)").bitcast(I32))
 
-        for q in range(4):
-            nc.sync.dma_start(
-                xs_tab[32 * q : 32 * q + 4 * PASSES, :].bitcast(I32),
-                x_scales[:, 4 * q : 4 * q + 4, :].bitcast(I32),
-            )
-        nc.sync.dma_start(offs_sb[:], offs)
+        def place_x_scales(g):
+            for r in range(4):
+                nc.sync.dma_start(
+                    xs_g[g][4 * g + r : P : 32, :].bitcast(I32),
+                    xs_c[64 * g + 4 * r : 64 * g + 64 : 16, :].bitcast(I32),
+                )
+
+        nc.sync.dma_start(xs_tab[0:P:4, :].bitcast(I32), x_scales.rearrange("g q n -> (g q) n").bitcast(I32))
         load_w(0)
+        nc.sync.dma_start(offs_sb[:], offs)
         load_w(1)
-        load_x(0)
+        x_tab = [sb([P, T], I32, "x_tab0")]
+        load_words(x_tab[0], x_words[0])
         nc.sync.dma_start(cen_sb[:], cen)
-        load_x(1)
-        for q in range(4):
-            nc.sync.dma_start(
-                es_tab[32 * q + ES_ROW : 32 * q + ES_ROW + 4, :].bitcast(I32),
-                e_scales[0, 4 * q : 4 * q + 4, :].bitcast(I32),
-            )
-        nc.sync.dma_start(e_tab[:], e_words[0].rearrange("p n r -> p (n r)").bitcast(I32))
-        nc.sync.dma_start(goal_sb[:], goal.rearrange("(c p) v -> p c v", p=P))
+        nc.sync.dma_start(es_tab[0:P:8, :].bitcast(I32), e_scales[0].bitcast(I32))
 
         ident = sb([P, P], F32, "ident")
         make_identity(nc, ident[:])
@@ -94,7 +92,6 @@ def tile_picked_ystrip_soft_p_kernel(
         def quant_w(g):
             nc.vector.quantize_mx(wq[g][:].bitcast(FP8X4), wq_s[g][:], w_bf[g][:])
 
-        xs_g = sb([P, S], U8, "xs_g")
         e_g = sb([P, S], U32, "e_g")
         x_g = [[sb([P, HALF], U32, f"x_g{g}_{u}") for u in range(2)] for g in range(PASSES)]
 
@@ -103,15 +100,40 @@ def tile_picked_ystrip_soft_p_kernel(
                 cols = slice(u * HALF // 16, (u + 1) * HALF // 16)
                 nc.vector.tensor_copy(x_g[g][u][:], x_tab[g][:].bitcast(U32).indirect(offs_sb[:, cols]))
 
-        nc.vector.tensor_copy(xs_g[:], xs_tab[:].indirect(offs_sb[:]))
+        nc.vector.tensor_copy(xs_c[:], xs_tab[:].indirect(offs_sb[:]))
+        place_x_scales(0)
+        x_tab.append(sb([P, T], I32, "x_tab1", tag="xs_tab"))
+        load_words(x_tab[1], x_words[1])
+        place_x_scales(1)
         cast_w(0)
         quant_w(0)
         cast_w(1)
+        e_tab = sb([P, W], I32, "e_tab", tag="w_raw1")
+        load_words(e_tab, e_words[0])
         quant_w(1)
         gather_x(0)
+        nc.vector.tensor_copy(es_c[:], es_tab[:].indirect(cen_sb[:]))
+        for r in range(4):
+            nc.sync.dma_start(es_g[ES_ROW + r : P : 32, :].bitcast(I32), es_c[8 * r : P : 32, :].bitcast(I32))
+        goal_sb = sb([P, CHUNKS, V], F32, "goal_sb", tag="es_tab")
+        nc.sync.dma_start(goal_sb[:], goal.rearrange("(c p) v -> p c v", p=P))
         gather_x(1)
-        es_g = sb([P, S], U8, "es_g")
-        nc.vector.tensor_copy(es_g[:], es_tab[:].indirect(cen_sb[:]))
+
+        warm_ps = bank(7, "warm_ps")
+
+        def warm_up(codes, scales):
+            nc.tensor.matmul_mx(
+                warm_ps[:].rearrange("p a b -> p (a b)"),
+                lhsT=codes.bitcast(FP8X4),
+                lhsT_scale=scales,
+                rhs=wq[1][:].bitcast(FP8X4),
+                rhs_scale=wq_s[1][:],
+                start=True,
+                stop=True,
+            )
+
+        for i in range(2):
+            warm_up(wq[1][:, 0:P], wq_s[1][:, 0:P])
 
         h_ps = [bank(c, f"h_ps{c}") for c in range(CHUNKS)]
         for g in range(PASSES):
@@ -122,7 +144,7 @@ def tile_picked_ystrip_soft_p_kernel(
                         lhsT=wq[g][:, j * P : (j + 1) * P].bitcast(FP8X4),
                         lhsT_scale=wq_s[g][:, j * P : (j + 1) * P],
                         rhs=x_g[g][c // 2][:, (c % 2) * P : (c % 2 + 1) * P].bitcast(FP8X4),
-                        rhs_scale=xs_g[4 * g : P, c * P : (c + 1) * P],
+                        rhs_scale=xs_g[g][4 * g : P, c * P : (c + 1) * P],
                         start=(g == 0 and j == 0),
                         stop=(g == PASSES - 1 and j == PACK - 1),
                     )
@@ -132,19 +154,23 @@ def tile_picked_ystrip_soft_p_kernel(
         for c in range(CHUNKS):
             dst = h_bf[c][:].rearrange("p (t j) -> p t j", j=PACK)
             src = h_ps[c][:].rearrange("p j t -> p t j")
-            nc.scalar.activation(dst, src, ACT.Copy)
+            if c == 0:
+                nc.vector.tensor_copy(dst, src)
+            else:
+                nc.scalar.activation(dst, src, ACT.Copy)
 
         def quant_h(c, codes):
             nc.vector.quantize_mx(codes.bitcast(FP8X4), hq_s[c][:], h_bf[c][:])
 
-        hq_early = sb([P, HALF], U32, "hq_early", tag="es_tab")
+        hq_early = sb([P, HALF], U32, "hq_early")
         hq = [hq_early[:, c * P : (c + 1) * P] for c in range(2)]
         for c in range(2):
             quant_h(c, hq[c])
+        warm_up(hq[0], hq_s[0][:])
         for u in range(2):
             cols = slice(u * HALF // 16, (u + 1) * HALF // 16)
             nc.vector.tensor_copy(e_g[:, u * HALF : (u + 1) * HALF], e_tab[:].bitcast(U32).indirect(cen_sb[:, cols]))
-        hq_late = sb([P, HALF], U32, "hq_late", tag="e_tab")
+        hq_late = sb([P, HALF], U32, "hq_late", tag="w_raw1")
         hq.extend(hq_late[:, c * P : (c + 1) * P] for c in range(2))
         for c in range(2, CHUNKS):
             quant_h(c, hq[c])

@@ -119,22 +119,6 @@ def tile_picked_ystrip_soft_p_kernel(
         nc.sync.dma_start(goal_sb[:], goal.rearrange("(c p) v -> p c v", p=P))
         gather_x(1)
 
-        warm_ps = bank(7, "warm_ps")
-
-        def warm_up(codes, scales):
-            nc.tensor.matmul_mx(
-                warm_ps[:].rearrange("p a b -> p (a b)"),
-                lhsT=codes.bitcast(FP8X4),
-                lhsT_scale=scales,
-                rhs=wq[1][:].bitcast(FP8X4),
-                rhs_scale=wq_s[1][:],
-                start=True,
-                stop=True,
-            )
-
-        for i in range(2):
-            warm_up(wq[1][:, 0:P], wq_s[1][:, 0:P])
-
         h_ps = [bank(c, f"h_ps{c}") for c in range(CHUNKS)]
         for g in range(PASSES):
             for c in range(CHUNKS):
@@ -166,7 +150,6 @@ def tile_picked_ystrip_soft_p_kernel(
         hq = [hq_early[:, c * P : (c + 1) * P] for c in range(2)]
         for c in range(2):
             quant_h(c, hq[c])
-        warm_up(hq[0], hq_s[0][:])
         for u in range(2):
             cols = slice(u * HALF // 16, (u + 1) * HALF // 16)
             nc.vector.tensor_copy(e_g[:, u * HALF : (u + 1) * HALF], e_tab[:].bitcast(U32).indirect(cen_sb[:, cols]))

@@ -23,7 +23,7 @@ PASSES = K // (P * PACK)
 CHUNKS = S // P
 HALF = S // 2
 ES_ROW = 8
-CAST_SPLIT = 64
+CAST_SPLIT = 96
 
 
 def tile_picked_ystrip_soft_p_kernel(
@@ -47,11 +47,12 @@ def tile_picked_ystrip_soft_p_kernel(
         es_tab = sb([P, W], U8, "es_tab")
         xs_c = sb([P, S], U8, "xs_c")
         es_c = sb([P, S], U8, "es_c")
-        xs_g = [sb([P, S], U8, f"xs_g{g}") for g in range(PASSES)]
-        es_g = sb([P, S], U8, "es_g")
+        xs_g = [sb([P, S], U8, "xs_g0")]
 
-        for plane in (xs_tab, es_tab, *xs_g, es_g):
-            nc.gpsimd.memset(plane[:].bitcast(I32), 0)
+        nc.gpsimd.memset(es_tab[:].bitcast(I32), 0)
+        nc.gpsimd.memset(xs_tab[64:P, :].bitcast(I32), 0)
+        nc.gpsimd.memset(xs_tab[32:64, :].bitcast(I32), 0)
+        nc.gpsimd.memset(xs_g[0][:].bitcast(I32), 0)
 
         def load_w(g):
             rows = w1[g * P * PACK : (g + 1) * P * PACK, :]
@@ -64,22 +65,20 @@ def tile_picked_ystrip_soft_p_kernel(
             for r in range(4):
                 nc.sync.dma_start(
                     xs_g[g][4 * g + r : P : 32, :].bitcast(I32),
-                    xs_c[64 * g + 4 * r : 64 * g + 64 : 16, :].bitcast(I32),
+                    xs_c[16 * g + r : 16 * g + 16 : 4, :].bitcast(I32),
                 )
 
-        nc.sync.dma_start(xs_tab[0:P:4, :].bitcast(I32), x_scales.rearrange("g q n -> (g q) n").bitcast(I32))
-        load_w(0)
+        nc.sync.dma_start(xs_tab[0:32, :].bitcast(I32), x_scales.rearrange("g q n -> (g q) n").bitcast(I32))
         nc.sync.dma_start(offs_sb[:], offs)
-        load_w(1)
-        x_tab = [sb([P, T], I32, "x_tab0")]
-        load_words(x_tab[0], x_words[0])
+        load_w(0)
         nc.sync.dma_start(cen_sb[:], cen)
         nc.sync.dma_start(es_tab[0:P:8, :].bitcast(I32), e_scales[0].bitcast(I32))
+        load_w(1)
 
         ident = sb([P, P], F32, "ident")
         make_identity(nc, ident[:])
 
-        wq = [sb([P, H], U32, f"wq{g}") for g in range(PASSES)]
+        wq = [sb([P, H], U32, "wq0")]
         wq_s = [sb([P, H], U8, f"wq_s{g}") for g in range(PASSES)]
         w_bf = [sb([P, H * PACK], BF16, f"w_bf{g}") for g in range(PASSES)]
 
@@ -102,20 +101,27 @@ def tile_picked_ystrip_soft_p_kernel(
 
         nc.vector.tensor_copy(xs_c[:], xs_tab[:].indirect(offs_sb[:]))
         place_x_scales(0)
-        x_tab.append(sb([P, T], I32, "x_tab1", tag="xs_tab"))
-        load_words(x_tab[1], x_words[1])
-        place_x_scales(1)
+        x_tab = [sb([P, T], I32, "x_tab0", tag="xs_tab")]
+        load_words(x_tab[0], x_words[0])
         cast_w(0)
-        quant_w(0)
-        cast_w(1)
-        e_tab = sb([P, W], I32, "e_tab", tag="w_raw1")
-        load_words(e_tab, e_words[0])
-        quant_w(1)
-        gather_x(0)
+        x_tab.append(sb([P, T], I32, "x_tab1", tag="w_raw0"))
+        load_words(x_tab[1], x_words[1])
         nc.vector.tensor_copy(es_c[:], es_tab[:].indirect(cen_sb[:]))
+        xs_g.append(sb([P, S], U8, "xs_g1", tag="es_tab"))
+        nc.gpsimd.memset(xs_g[1][:].bitcast(I32), 0)
+        place_x_scales(1)
+        quant_w(0)
+        e_tab = sb([P, W], I32, "e_tab", tag="w_bf0")
+        load_words(e_tab, e_words[0])
+        cast_w(1)
+        es_g = sb([P, S], U8, "es_g", tag="w_raw1")
+        nc.gpsimd.memset(es_g[:].bitcast(I32), 0)
         for r in range(4):
             nc.sync.dma_start(es_g[ES_ROW + r : P : 32, :].bitcast(I32), es_c[8 * r : P : 32, :].bitcast(I32))
-        goal_sb = sb([P, CHUNKS, V], F32, "goal_sb", tag="es_tab")
+        gather_x(0)
+        wq.append(sb([P, H], U32, "wq1", tag="xs_tab"))
+        quant_w(1)
+        goal_sb = sb([P, CHUNKS, V], F32, "goal_sb", tag="w_bf1")
         nc.sync.dma_start(goal_sb[:], goal.rearrange("(c p) v -> p c v", p=P))
         gather_x(1)
 
@@ -153,7 +159,7 @@ def tile_picked_ystrip_soft_p_kernel(
         for u in range(2):
             cols = slice(u * HALF // 16, (u + 1) * HALF // 16)
             nc.vector.tensor_copy(e_g[:, u * HALF : (u + 1) * HALF], e_tab[:].bitcast(U32).indirect(cen_sb[:, cols]))
-        hq_late = sb([P, HALF], U32, "hq_late", tag="w_raw1")
+        hq_late = sb([P, HALF], U32, "hq_late", tag="w_bf0")
         hq.extend(hq_late[:, c * P : (c + 1) * P] for c in range(2))
         for c in range(2, CHUNKS):
             quant_h(c, hq[c])

@@ -23,7 +23,7 @@ PASSES = K // (P * PACK)
 CHUNKS = S // P
 HALF = S // 2
 ES_ROW = 8
-CAST_SPLIT = 96
+CAST_SPLIT = (96, 64)
 
 
 def tile_picked_ystrip_soft_p_kernel(
@@ -52,7 +52,7 @@ def tile_picked_ystrip_soft_p_kernel(
         nc.gpsimd.memset(es_tab[:].bitcast(I32), 0)
         nc.gpsimd.memset(xs_tab[64:P, :].bitcast(I32), 0)
         nc.gpsimd.memset(xs_tab[32:64, :].bitcast(I32), 0)
-        nc.gpsimd.memset(xs_g[0][:].bitcast(I32), 0)
+        nc.vector.memset(xs_g[0][:].bitcast(I32), 0)
 
         def load_w(g):
             rows = w1[g * P * PACK : (g + 1) * P * PACK, :]
@@ -78,18 +78,23 @@ def tile_picked_ystrip_soft_p_kernel(
         ident = sb([P, P], F32, "ident")
         make_identity(nc, ident[:])
 
-        wq = [sb([P, H], U32, "wq0")]
+        wq = [sb([P, H], U32, f"wq{g}") for g in range(PASSES)]
         wq_s = [sb([P, H], U8, f"wq_s{g}") for g in range(PASSES)]
         w_bf = [sb([P, H * PACK], BF16, f"w_bf{g}") for g in range(PASSES)]
 
         def cast_w(g):
             dst = w_bf[g][:].rearrange("p (t m j) -> p m t j", t=PACK, j=PACK)
             src = w_raw[g][:].rearrange("p j (m t) -> p m t j", t=PACK)
-            nc.scalar.activation(dst[:, :CAST_SPLIT], src[:, :CAST_SPLIT], ACT.Copy)
-            nc.vector.tensor_copy(dst[:, CAST_SPLIT:], src[:, CAST_SPLIT:])
+            split = CAST_SPLIT[g]
+            nc.scalar.activation(dst[:, :split], src[:, :split], ACT.Copy)
+            nc.vector.tensor_copy(dst[:, split:], src[:, split:])
 
         def quant_w(g):
-            nc.vector.quantize_mx(wq[g][:].bitcast(FP8X4), wq_s[g][:], w_bf[g][:])
+            for u in range(2):
+                cols = slice(u * H // 2, (u + 1) * H // 2)
+                nc.vector.quantize_mx(
+                    wq[g][:, cols].bitcast(FP8X4), wq_s[g][:, cols], w_bf[g][:, u * 2 * H : (u + 1) * 2 * H]
+                )
 
         e_g = sb([P, S], U32, "e_g")
         x_g = [[sb([P, HALF], U32, f"x_g{g}_{u}") for u in range(2)] for g in range(PASSES)]
@@ -108,22 +113,33 @@ def tile_picked_ystrip_soft_p_kernel(
         load_words(x_tab[1], x_words[1])
         nc.vector.tensor_copy(es_c[:], es_tab[:].indirect(cen_sb[:]))
         xs_g.append(sb([P, S], U8, "xs_g1", tag="es_tab"))
-        nc.gpsimd.memset(xs_g[1][:].bitcast(I32), 0)
+        nc.vector.memset(xs_g[1][:].bitcast(I32), 0)
         place_x_scales(1)
         quant_w(0)
         e_tab = sb([P, W], I32, "e_tab", tag="w_bf0")
         load_words(e_tab, e_words[0])
         cast_w(1)
         es_g = sb([P, S], U8, "es_g", tag="w_raw1")
-        nc.gpsimd.memset(es_g[:].bitcast(I32), 0)
+        nc.vector.memset(es_g[:].bitcast(I32), 0)
         for r in range(4):
             nc.sync.dma_start(es_g[ES_ROW + r : P : 32, :].bitcast(I32), es_c[8 * r : P : 32, :].bitcast(I32))
-        gather_x(0)
-        wq.append(sb([P, H], U32, "wq1", tag="xs_tab"))
         quant_w(1)
         goal_sb = sb([P, CHUNKS, V], F32, "goal_sb", tag="w_bf1")
         nc.sync.dma_start(goal_sb[:], goal.rearrange("(c p) v -> p c v", p=P))
+        gather_x(0)
         gather_x(1)
+
+        warm = psum.tile([P, H], F32, name="warm", tag="bank7")
+        for n in range(3):
+            nc.tensor.matmul_mx(
+                warm[:],
+                lhsT=wq[1][:, :P].bitcast(FP8X4),
+                lhsT_scale=wq_s[1][:, :P],
+                rhs=wq[0][:].bitcast(FP8X4),
+                rhs_scale=wq_s[0][:],
+                start=True,
+                stop=True,
+            )
 
         h_ps = [bank(c, f"h_ps{c}") for c in range(CHUNKS)]
         for g in range(PASSES):
@@ -159,7 +175,7 @@ def tile_picked_ystrip_soft_p_kernel(
         for u in range(2):
             cols = slice(u * HALF // 16, (u + 1) * HALF // 16)
             nc.vector.tensor_copy(e_g[:, u * HALF : (u + 1) * HALF], e_tab[:].bitcast(U32).indirect(cen_sb[:, cols]))
-        hq_late = sb([P, HALF], U32, "hq_late", tag="w_bf0")
+        hq_late = sb([P, HALF], U32, "hq_late", tag="es_c")
         hq.extend(hq_late[:, c * P : (c + 1) * P] for c in range(2))
         for c in range(2, CHUNKS):
             quant_h(c, hq[c])

@@ -130,7 +130,7 @@ def tile_picked_ystrip_soft_p_kernel(
         gather_x(1)
 
         warm = psum.tile([P, H], F32, name="warm", tag="bank7")
-        for n in range(3):
+        for n in range(2):
             nc.tensor.matmul_mx(
                 warm[:],
                 lhsT=wq[1][:, :P].bitcast(FP8X4),
@@ -172,6 +172,16 @@ def tile_picked_ystrip_soft_p_kernel(
         hq = [hq_early[:, c * P : (c + 1) * P] for c in range(2)]
         for c in range(2):
             quant_h(c, hq[c])
+        bridge = psum.tile([P, H], F32, name="bridge", tag="bank7")
+        nc.tensor.matmul_mx(
+            bridge[:],
+            lhsT=hq[0].bitcast(FP8X4),
+            lhsT_scale=hq_s[0][:],
+            rhs=wq[0][:].bitcast(FP8X4),
+            rhs_scale=wq_s[0][:],
+            start=True,
+            stop=True,
+        )
         for u in range(2):
             cols = slice(u * HALF // 16, (u + 1) * HALF // 16)
             nc.vector.tensor_copy(e_g[:, u * HALF : (u + 1) * HALF], e_tab[:].bitcast(U32).indirect(cen_sb[:, cols]))

@@ -142,18 +142,23 @@ def tile_picked_ystrip_soft_p_kernel(
             )
 
         h_ps = [bank(c, f"h_ps{c}") for c in range(CHUNKS)]
+        def project(c, g, first, last):
+            for j in range(PACK):
+                nc.tensor.matmul_mx(
+                    h_ps[c][:, j, :],
+                    lhsT=wq[g][:, j * P : (j + 1) * P].bitcast(FP8X4),
+                    lhsT_scale=wq_s[g][:, j * P : (j + 1) * P],
+                    rhs=x_g[g][c // 2][:, (c % 2) * P : (c % 2 + 1) * P].bitcast(FP8X4),
+                    rhs_scale=xs_g[g][4 * g : P, c * P : (c + 1) * P],
+                    start=(first and j == 0),
+                    stop=(last and j == PACK - 1),
+                )
+
         for g in range(PASSES):
-            for c in range(CHUNKS):
-                for j in range(PACK):
-                    nc.tensor.matmul_mx(
-                        h_ps[c][:, j, :],
-                        lhsT=wq[g][:, j * P : (j + 1) * P].bitcast(FP8X4),
-                        lhsT_scale=wq_s[g][:, j * P : (j + 1) * P],
-                        rhs=x_g[g][c // 2][:, (c % 2) * P : (c % 2 + 1) * P].bitcast(FP8X4),
-                        rhs_scale=xs_g[g][4 * g : P, c * P : (c + 1) * P],
-                        start=(g == 0 and j == 0),
-                        stop=(g == PASSES - 1 and j == PACK - 1),
-                    )
+            for c in range(CHUNKS - 1):
+                project(c, g, g == 0, g == PASSES - 1)
+        for g in reversed(range(PASSES)):
+            project(CHUNKS - 1, g, g == PASSES - 1, g == 0)
 
         h_bf = [sb([P, P * PACK], BF16, f"h_bf{c}") for c in range(CHUNKS)]
         hq_s = [sb([P, P], U8, f"hq_s{c}") for c in range(CHUNKS)]
@@ -244,7 +249,7 @@ def tile_picked_ystrip_soft_p_kernel(
         prob = [sb([P, V], F32, f"prob{c}") for c in range(CHUNKS)]
         tot = [sb([P, 1], F32, f"tot{c}") for c in range(CHUNKS)]
         inv = [sb([P, 1], F32, f"inv{c}") for c in range(CHUNKS)]
-        res = [sb([P, V], F32, f"res{c}") for c in range(CHUNKS)]
+        res = [sb([P, 2, V], F32, f"res{u}") for u in range(2)]
         neg = [psum.tile([P, V], F32, name=f"neg{c}", tag=f"bank{4 + c}") for c in range(CHUNKS)]
         for c in range(CHUNKS):
             turn(neg[c][:], margin[:, c, :], True, False)
@@ -266,5 +271,8 @@ def tile_picked_ystrip_soft_p_kernel(
             if c < CHUNKS:
                 nc.vector.reciprocal(inv[c][:], tot[c][:])
             if c > 0:
-                nc.vector.tensor_scalar(res[c - 1][:], prob[c - 1][:], inv[c - 1][:], None, ALU.mult)
-                nc.sync.dma_start(out[(c - 1) * P : c * P, :], res[c - 1][:])
+                u, n = divmod(c - 1, 2)
+                nc.vector.tensor_scalar(res[u][:, n, :], prob[c - 1][:], inv[c - 1][:], None, ALU.mult)
+                if n == 1:
+                    rows = out[u * HALF : (u + 1) * HALF, :]
+                    nc.sync.dma_start(rows.rearrange("(n p) v -> p n v", p=P), res[u][:])

@@ -234,34 +234,41 @@ def tile_picked_ystrip_soft_p_kernel(
         margin = sb([P, CHUNKS, P], F32, "margin")
         nc.vector.tensor_scalar(margin[:], goal_ps[:], 0.9, None, ALU.mult)
 
-        se_ps = bank(0, "se_ps")
+        se_first = psum.tile([P, P], F32, name="se_first", tag="bank4")
+        se_rest = psum.tile([P, CHUNKS - 1, P], F32, name="se_rest", tag="bank0")
+        se_ps = [se_first[:]] + [se_rest[:, c, :] for c in range(CHUNKS - 1)]
         ses_ps = [psum.tile([P, 2, P], F32, name=f"ses_ps{u}", tag=f"bank{1 + u}") for u in range(2)]
         for c in range(CHUNKS):
-            sum_turned(se_ps[:, c, :], ex[c][:])
+            sum_turned(se_ps[c], ex[c][:])
             if c > 0:
                 sum_turned(ses_ps[(c - 1) // 2][:, (c - 1) % 2, :], es[c - 1][:])
         sum_turned(ses_ps[1][:, 1, :], es[CHUNKS - 1][:])
 
-        rs = [sb([P, P], F32, f"rs{c}") for c in range(CHUNKS)]
+        rs_late = sb([P, 2, P], F32, "rs_late")
+        rs = [sb([P, P], F32, f"rs{c}") for c in range(2)] + [rs_late[:, u, :] for u in range(2)]
         part = [sb([P, P], F32, f"part{c}") for c in range(CHUNKS)]
         t3 = [sb([P, P], F32, f"t3_{c}") for c in range(CHUNKS)]
-        low = [sb([P, 1], F32, f"low{c}") for c in range(CHUNKS)]
         prob = [sb([P, V], F32, f"prob{c}") for c in range(CHUNKS)]
         tot = [sb([P, 1], F32, f"tot{c}") for c in range(CHUNKS)]
         inv = [sb([P, 1], F32, f"inv{c}") for c in range(CHUNKS)]
         res = [sb([P, 2, V], F32, f"res{u}") for u in range(2)]
-        neg = [psum.tile([P, V], F32, name=f"neg{c}", tag=f"bank{4 + c}") for c in range(CHUNKS)]
+        neg = [psum.tile([P, V], F32, name=f"neg{c}", tag=f"bank{(5, 6, 7, 3)[c]}") for c in range(CHUNKS)]
         for c in range(CHUNKS):
             turn(neg[c][:], margin[:, c, :], True, False)
-        for c in range(CHUNKS):
-            nc.scalar.activation(rs[c][:], se_ps[:, c, :], ACT.Abs_reciprocal_sqrt)
-        for c in range(CHUNKS + 1):
+        nc.vector.reciprocal(rs[0][:], se_ps[0])
+        nc.scalar.activation(rs[1][:], se_ps[1], ACT.Abs_reciprocal_sqrt)
+        nc.scalar.activation(rs_late[:], se_rest[:, 1:, :], ACT.Abs_reciprocal_sqrt)
+        for c in range(1, CHUNKS + 1):
             if c < CHUNKS:
                 nc.vector.scalar_tensor_tensor(
                     part[c][:], ses_ps[c // 2][:, c % 2, :], -3.0, rs[c][:], ALU.mult, ALU.mult
                 )
-            if c > 0:
-                nc.vector.tensor_tensor(t3[c - 1][:], part[c - 1][:], rs[c - 1][:], ALU.mult)
+            if c == 1:
+                nc.vector.scalar_tensor_tensor(t3[0][:], ses_ps[0][:, 0, :], -3.0, rs[0][:], ALU.mult, ALU.mult)
+            if c > 1:
+                engine = nc.gpsimd if c == 2 else nc.vector
+                engine.tensor_tensor(t3[c - 1][:], part[c - 1][:], rs[c - 1][:], ALU.mult)
+        low = [sb([P, 1], F32, f"low{c}") for c in range(CHUNKS)]
         for c in range(CHUNKS):
             turn(neg[c][:], t3[c][:], False, True)
             nc.vector.tensor_reduce(low[c][:], neg[c][:], AX.X, ALU.min)

@@ -97,12 +97,18 @@ def tile_picked_ystrip_soft_p_kernel(
                 )
 
         e_g = sb([P, S], U32, "e_g")
-        x_g = [[sb([P, HALF], U32, f"x_g{g}_{u}") for u in range(2)] for g in range(PASSES)]
+        x_width = (HALF, P)
+        x_g = [[sb([P, n], U32, f"x_g{g}_{u}") for u in range(S // n)] for g, n in enumerate(x_width)]
 
         def gather_x(g):
-            for u in range(2):
-                cols = slice(u * HALF // 16, (u + 1) * HALF // 16)
+            n = x_width[g]
+            for u in range(S // n):
+                cols = slice(u * n // 16, (u + 1) * n // 16)
                 nc.vector.tensor_copy(x_g[g][u][:], x_tab[g][:].bitcast(U32).indirect(offs_sb[:, cols]))
+
+        def x_codes(g, c):
+            u, first = divmod(c * P, x_width[g])
+            return x_g[g][u][:, first : first + P]
 
         nc.vector.tensor_copy(xs_c[:], xs_tab[:].indirect(offs_sb[:]))
         place_x_scales(0)
@@ -148,7 +154,7 @@ def tile_picked_ystrip_soft_p_kernel(
                     h_ps[c][:, j, :],
                     lhsT=wq[g][:, j * P : (j + 1) * P].bitcast(FP8X4),
                     lhsT_scale=wq_s[g][:, j * P : (j + 1) * P],
-                    rhs=x_g[g][c // 2][:, (c % 2) * P : (c % 2 + 1) * P].bitcast(FP8X4),
+                    rhs=x_codes(g, c).bitcast(FP8X4),
                     rhs_scale=xs_g[g][4 * g : P, c * P : (c + 1) * P],
                     start=(first and j == 0),
                     stop=(last and j == PACK - 1),
@@ -165,7 +171,7 @@ def tile_picked_ystrip_soft_p_kernel(
         for c in range(CHUNKS):
             dst = h_bf[c][:].rearrange("p (t j) -> p t j", j=PACK)
             src = h_ps[c][:].rearrange("p j t -> p t j")
-            if c == 0:
+            if c == 1:
                 nc.vector.tensor_copy(dst, src)
             else:
                 nc.scalar.activation(dst, src, ACT.Copy)
@@ -187,9 +193,9 @@ def tile_picked_ystrip_soft_p_kernel(
             start=True,
             stop=True,
         )
-        for u in range(2):
-            cols = slice(u * HALF // 16, (u + 1) * HALF // 16)
-            nc.vector.tensor_copy(e_g[:, u * HALF : (u + 1) * HALF], e_tab[:].bitcast(U32).indirect(cen_sb[:, cols]))
+        for u in range(4):
+            cols = slice(u * P // 16, (u + 1) * P // 16)
+            nc.vector.tensor_copy(e_g[:, u * P : (u + 1) * P], e_tab[:].bitcast(U32).indirect(cen_sb[:, cols]))
         hq_late = sb([P, HALF], U32, "hq_late", tag="es_c")
         hq.extend(hq_late[:, c * P : (c + 1) * P] for c in range(2))
         for c in range(2, CHUNKS):
@@ -202,31 +208,34 @@ def tile_picked_ystrip_soft_p_kernel(
             for d in range(D):
                 turn(dst, src[:, d, :], d == 0, d == D - 1)
 
-        ex = [sb([P, D, V], F32, f"ex{c}") for c in range(CHUNKS)]
-        es = [sb([P, D, V], F32, f"es{c}") for c in range(CHUNKS)]
+        ex_pair = [sb([P, 2, D, V], F32, f"ex{n}") for n in range(2)]
+        es_pair = [sb([P, 2, D, V], F32, f"es{n}") for n in range(2)]
+        ex = [ex_pair[c // 2][:, c % 2, :, :] for c in range(CHUNKS)]
+        es = [es_pair[c // 2][:, c % 2, :, :] for c in range(CHUNKS)]
 
-        def similarity(c, n, first, width):
-            y_ps = psum.tile([P, width], F32, name=f"y_ps{c}_{first}", tag=f"bank{n}")
-            nc.tensor.matmul_mx(
-                y_ps[:],
-                lhsT=hq[c].bitcast(FP8X4),
-                lhsT_scale=hq_s[c][:],
-                rhs=e_g[:, first : first + width].bitcast(FP8X4),
-                rhs_scale=es_g[ES_ROW:P, first : first + width],
-                start=True,
-                stop=True,
-            )
-            y_dv = y_ps[:].rearrange("p (v d) -> p d v", d=D)
+        def similarity(n, chunks, first, width):
+            y_ps = psum.tile([P, len(chunks), width], F32, name=f"y_ps{n}", tag=f"bank{n}")
+            for i, c in enumerate(chunks):
+                nc.tensor.matmul_mx(
+                    y_ps[:, i, :],
+                    lhsT=hq[c].bitcast(FP8X4),
+                    lhsT_scale=hq_s[c][:],
+                    rhs=e_g[:, first : first + width].bitcast(FP8X4),
+                    rhs_scale=es_g[ES_ROW:P, first : first + width],
+                    start=True,
+                    stop=True,
+                )
+            y_dv = y_ps[:].rearrange("p c (v d) -> p c d v", d=D)
+            pair = slice(chunks[0] % 2, chunks[-1] % 2 + 1)
             classes = slice(first // D, (first + width) // D)
-            nc.scalar.activation(ex[c][:, :, classes], y_dv, ACT.Exp, scale=2.0)
-            nc.vector.tensor_tensor(es[c][:, :, classes], y_dv, ex[c][:, :, classes], ALU.mult)
+            ex_part = ex_pair[chunks[0] // 2][:, pair, :, classes]
+            nc.scalar.activation(ex_part, y_dv, ACT.Exp, scale=2.0)
+            nc.vector.tensor_tensor(es_pair[chunks[0] // 2][:, pair, :, classes], y_dv, ex_part, ALU.mult)
 
-        for c in range(2):
-            similarity(c, 4 + c, 0, HALF)
-        for c in range(2):
-            similarity(c, 1 + c, HALF, HALF)
+        for u in range(4):
+            similarity((4, 5, 0, 1)[u], (0, 1), u * P, P)
         for c in range(2, CHUNKS):
-            similarity(c, 4 + c, 0, S)
+            similarity(4 + c, (c,), 0, S)
 
         goal_ps = bank(3, "goal_ps")
         for c in range(CHUNKS):
@@ -235,14 +244,14 @@ def tile_picked_ystrip_soft_p_kernel(
         nc.vector.tensor_scalar(margin[:], goal_ps[:], 0.9, None, ALU.mult)
 
         se_first = psum.tile([P, P], F32, name="se_first", tag="bank4")
-        se_rest = psum.tile([P, CHUNKS - 1, P], F32, name="se_rest", tag="bank0")
+        se_rest = psum.tile([P, CHUNKS - 1, P], F32, name="se_rest", tag="bank2")
         se_ps = [se_first[:]] + [se_rest[:, c, :] for c in range(CHUNKS - 1)]
-        ses_ps = [psum.tile([P, 2, P], F32, name=f"ses_ps{u}", tag=f"bank{1 + u}") for u in range(2)]
+        ses_ps = [psum.tile([P, 2, P], F32, name=f"ses_ps{u}", tag=f"bank{(5, 0)[u]}") for u in range(2)]
         for c in range(CHUNKS):
-            sum_turned(se_ps[c], ex[c][:])
+            sum_turned(se_ps[c], ex[c])
             if c > 0:
-                sum_turned(ses_ps[(c - 1) // 2][:, (c - 1) % 2, :], es[c - 1][:])
-        sum_turned(ses_ps[1][:, 1, :], es[CHUNKS - 1][:])
+                sum_turned(ses_ps[(c - 1) // 2][:, (c - 1) % 2, :], es[c - 1])
+        sum_turned(ses_ps[1][:, 1, :], es[CHUNKS - 1])
 
         rs_late = sb([P, 2, P], F32, "rs_late")
         rs = [sb([P, P], F32, f"rs{c}") for c in range(2)] + [rs_late[:, u, :] for u in range(2)]
@@ -252,7 +261,7 @@ def tile_picked_ystrip_soft_p_kernel(
         tot = [sb([P, 1], F32, f"tot{c}") for c in range(CHUNKS)]
         inv = [sb([P, 1], F32, f"inv{c}") for c in range(CHUNKS)]
         res = [sb([P, 2, V], F32, f"res{u}") for u in range(2)]
-        neg = [psum.tile([P, V], F32, name=f"neg{c}", tag=f"bank{(5, 6, 7, 3)[c]}") for c in range(CHUNKS)]
+        neg = [psum.tile([P, V], F32, name=f"neg{c}", tag=f"bank{(1, 6, 7, 3)[c]}") for c in range(CHUNKS)]
         for c in range(CHUNKS):
             turn(neg[c][:], margin[:, c, :], True, False)
         nc.vector.reciprocal(rs[0][:], se_ps[0])

@@ -1,3 +1,4 @@
+import math
 from contextlib import ExitStack
 
 import concourse.mybir as mybir
@@ -23,6 +24,7 @@ PASSES = K // (P * PACK)
 CHUNKS = S // P
 HALF = S // 2
 ES_ROW = 8
+LN2 = math.log(2.0)
 CAST_SPLIT = (96, 64)
 
 
@@ -213,6 +215,8 @@ def tile_picked_ystrip_soft_p_kernel(
         ex = [ex_pair[c // 2][:, c % 2, :, :] for c in range(CHUNKS)]
         es = [es_pair[c // 2][:, c % 2, :, :] for c in range(CHUNKS)]
 
+        mass = sb([P, 2], F32, "mass")
+
         def similarity(n, chunks, first, width):
             y_ps = psum.tile([P, len(chunks), width], F32, name=f"y_ps{n}", tag=f"bank{n}")
             for i, c in enumerate(chunks):
@@ -229,7 +233,8 @@ def tile_picked_ystrip_soft_p_kernel(
             pair = slice(chunks[0] % 2, chunks[-1] % 2 + 1)
             classes = slice(first // D, (first + width) // D)
             ex_part = ex_pair[chunks[0] // 2][:, pair, :, classes]
-            nc.scalar.activation(ex_part, y_dv, ACT.Exp, scale=2.0)
+            row_sum = mass[:, chunks[0] - 2 : chunks[0] - 1] if width == S else None
+            nc.scalar.activation(ex_part, y_dv, ACT.Exp, scale=2.0, accum_out=row_sum)
             nc.vector.tensor_tensor(es_pair[chunks[0] // 2][:, pair, :, classes], y_dv, ex_part, ALU.mult)
 
         for u in range(4):
@@ -277,12 +282,15 @@ def tile_picked_ystrip_soft_p_kernel(
             if c > 1:
                 engine = nc.gpsimd if c == 2 else nc.vector
                 engine.tensor_tensor(t3[c - 1][:], part[c - 1][:], rs[c - 1][:], ALU.mult)
-        low = [sb([P, 1], F32, f"low{c}") for c in range(CHUNKS)]
+        shift = sb([P, 2], F32, "shift")
+        nc.vector.tensor_scalar(shift[:], mass[:].bitcast(I32), -1.5 * LN2 / 2**23, 1.5 * LN2 * 127, ALU.mult, ALU.add)
+        low = [sb([P, 1], F32, f"low{c}")[:] for c in range(2)] + [shift[:, u : u + 1] for u in range(2)]
         for c in range(CHUNKS):
             turn(neg[c][:], t3[c][:], False, True)
-            nc.vector.tensor_reduce(low[c][:], neg[c][:], AX.X, ALU.min)
+            if c < 2:
+                nc.vector.tensor_reduce(low[c], neg[c][:], AX.X, ALU.min)
         for c in range(CHUNKS):
-            nc.scalar.activation(prob[c][:], neg[c][:], ACT.Exp, bias=low[c][:], scale=-1.0, accum_out=tot[c][:])
+            nc.scalar.activation(prob[c][:], neg[c][:], ACT.Exp, bias=low[c], scale=-1.0, accum_out=tot[c][:])
         for c in range(CHUNKS + 1):
             if c < CHUNKS:
                 nc.vector.reciprocal(inv[c][:], tot[c][:])

@@ -74,7 +74,7 @@ def tile_picked_ystrip_soft_p_kernel(
         nc.sync.dma_start(offs_sb[:], offs)
         load_w(0)
         nc.sync.dma_start(cen_sb[:], cen)
-        nc.sync.dma_start(es_tab[0:P:8, :].bitcast(I32), e_scales[0].bitcast(I32))
+        nc.sync.dma_start(es_tab[64:P:4, :].bitcast(I32), e_scales[0].bitcast(I32))
         load_w(1)
 
         ident = sb([P, P], F32, "ident")
@@ -130,7 +130,7 @@ def tile_picked_ystrip_soft_p_kernel(
         es_g = sb([P, S], U8, "es_g", tag="w_raw1")
         nc.vector.memset(es_g[:].bitcast(I32), 0)
         for r in range(4):
-            nc.sync.dma_start(es_g[ES_ROW + r : P : 32, :].bitcast(I32), es_c[8 * r : P : 32, :].bitcast(I32))
+            nc.sync.dma_start(es_g[ES_ROW + r : P : 32, :].bitcast(I32), es_c[64 + 4 * r : P : 16, :].bitcast(I32))
         quant_w(1)
         goal_sb = sb([P, CHUNKS, V], F32, "goal_sb", tag="w_bf1")
         nc.sync.dma_start(goal_sb[:], goal.rearrange("(c p) v -> p c v", p=P))

@@ -23,7 +23,7 @@ PACK = 4
 PASSES = K // (P * PACK)
 CHUNKS = S // P
 HALF = S // 2
-ES_ROW = 8
+ES_ROW = 12
 LN2 = math.log(2.0)
 CAST_SPLIT = (96, 64)
 
@@ -66,7 +66,7 @@ def tile_picked_ystrip_soft_p_kernel(
         def place_x_scales(g):
             for r in range(4):
                 nc.sync.dma_start(
-                    xs_g[g][4 * g + r : P : 32, :].bitcast(I32),
+                    xs_g[g][8 * g + r : P : 32, :].bitcast(I32),
                     xs_c[16 * g + r : 16 * g + 16 : 4, :].bitcast(I32),
                 )
 
@@ -74,7 +74,7 @@ def tile_picked_ystrip_soft_p_kernel(
         nc.sync.dma_start(offs_sb[:], offs)
         load_w(0)
         nc.sync.dma_start(cen_sb[:], cen)
-        nc.sync.dma_start(es_tab[64:P:4, :].bitcast(I32), e_scales[0].bitcast(I32))
+        nc.sync.dma_start(es_tab[4:P:8, :].bitcast(I32), e_scales[0].bitcast(I32))
         load_w(1)
 
         ident = sb([P, P], F32, "ident")
@@ -99,7 +99,7 @@ def tile_picked_ystrip_soft_p_kernel(
                 )
 
         e_g = sb([P, S], U32, "e_g")
-        x_width = (HALF, P)
+        x_width = (P, P)
         x_g = [[sb([P, n], U32, f"x_g{g}_{u}") for u in range(S // n)] for g, n in enumerate(x_width)]
 
         def gather_x(g):
@@ -130,7 +130,7 @@ def tile_picked_ystrip_soft_p_kernel(
         es_g = sb([P, S], U8, "es_g", tag="w_raw1")
         nc.vector.memset(es_g[:].bitcast(I32), 0)
         for r in range(4):
-            nc.sync.dma_start(es_g[ES_ROW + r : P : 32, :].bitcast(I32), es_c[64 + 4 * r : P : 16, :].bitcast(I32))
+            nc.sync.dma_start(es_g[ES_ROW + r : P : 32, :].bitcast(I32), es_c[4 + 8 * r : P : 32, :].bitcast(I32))
         quant_w(1)
         goal_sb = sb([P, CHUNKS, V], F32, "goal_sb", tag="w_bf1")
         nc.sync.dma_start(goal_sb[:], goal.rearrange("(c p) v -> p c v", p=P))
@@ -138,16 +138,15 @@ def tile_picked_ystrip_soft_p_kernel(
         gather_x(1)
 
         warm = psum.tile([P, H], F32, name="warm", tag="bank7")
-        for n in range(2):
-            nc.tensor.matmul_mx(
-                warm[:],
-                lhsT=wq[1][:, :P].bitcast(FP8X4),
-                lhsT_scale=wq_s[1][:, :P],
-                rhs=wq[0][:].bitcast(FP8X4),
-                rhs_scale=wq_s[0][:],
-                start=True,
-                stop=True,
-            )
+        nc.tensor.matmul_mx(
+            warm[:],
+            lhsT=wq[1][:, :P].bitcast(FP8X4),
+            lhsT_scale=wq_s[1][:, :P],
+            rhs=wq[0][:].bitcast(FP8X4),
+            rhs_scale=wq_s[0][:],
+            start=True,
+            stop=True,
+        )
 
         h_ps = [bank(c, f"h_ps{c}") for c in range(CHUNKS)]
         def project(c, g, first, last):
@@ -157,7 +156,7 @@ def tile_picked_ystrip_soft_p_kernel(
                     lhsT=wq[g][:, j * P : (j + 1) * P].bitcast(FP8X4),
                     lhsT_scale=wq_s[g][:, j * P : (j + 1) * P],
                     rhs=x_codes(g, c).bitcast(FP8X4),
-                    rhs_scale=xs_g[g][4 * g : P, c * P : (c + 1) * P],
+                    rhs_scale=xs_g[g][8 * g : P, c * P : (c + 1) * P],
                     start=(first and j == 0),
                     stop=(last and j == PACK - 1),
                 )
@@ -185,16 +184,6 @@ def tile_picked_ystrip_soft_p_kernel(
         hq = [hq_early[:, c * P : (c + 1) * P] for c in range(2)]
         for c in range(2):
             quant_h(c, hq[c])
-        bridge = psum.tile([P, H], F32, name="bridge", tag="bank7")
-        nc.tensor.matmul_mx(
-            bridge[:],
-            lhsT=hq[0].bitcast(FP8X4),
-            lhsT_scale=hq_s[0][:],
-            rhs=wq[0][:].bitcast(FP8X4),
-            rhs_scale=wq_s[0][:],
-            start=True,
-            stop=True,
-        )
         for u in range(4):
             cols = slice(u * P // 16, (u + 1) * P // 16)
             nc.vector.tensor_copy(e_g[:, u * P : (u + 1) * P], e_tab[:].bitcast(U32).indirect(cen_sb[:, cols]))

@@ -25,7 +25,7 @@ CHUNKS = S // P
 HALF = S // 2
 ES_ROW = 12
 LN2 = math.log(2.0)
-CAST_SPLIT = (96, 64)
+CAST_SPLIT = (64, 48)
 
 
 def tile_picked_ystrip_soft_p_kernel(

@@ -1,4 +1,3 @@
-import math
 from contextlib import ExitStack
 
 import concourse.mybir as mybir
@@ -24,7 +23,6 @@ PASSES = K // (P * PACK)
 CHUNKS = S // P
 HALF = S // 2
 ES_ROW = 12
-LN2 = math.log(2.0)
 CAST_SPLIT = (64, 48)
 
 
@@ -204,8 +202,6 @@ def tile_picked_ystrip_soft_p_kernel(
         ex = [ex_pair[c // 2][:, c % 2, :, :] for c in range(CHUNKS)]
         es = [es_pair[c // 2][:, c % 2, :, :] for c in range(CHUNKS)]
 
-        mass = sb([P, 2], F32, "mass")
-
         def similarity(n, chunks, first, width):
             y_ps = psum.tile([P, len(chunks), width], F32, name=f"y_ps{n}", tag=f"bank{n}")
             for i, c in enumerate(chunks):
@@ -222,8 +218,7 @@ def tile_picked_ystrip_soft_p_kernel(
             pair = slice(chunks[0] % 2, chunks[-1] % 2 + 1)
             classes = slice(first // D, (first + width) // D)
             ex_part = ex_pair[chunks[0] // 2][:, pair, :, classes]
-            row_sum = mass[:, chunks[0] - 2 : chunks[0] - 1] if width == S else None
-            nc.scalar.activation(ex_part, y_dv, ACT.Exp, scale=2.0, accum_out=row_sum)
+            nc.scalar.activation(ex_part, y_dv, ACT.Exp, scale=2.0)
             nc.vector.tensor_tensor(es_pair[chunks[0] // 2][:, pair, :, classes], y_dv, ex_part, ALU.mult)
 
         for u in range(4):
@@ -271,15 +266,12 @@ def tile_picked_ystrip_soft_p_kernel(
             if c > 1:
                 engine = nc.gpsimd if c == 2 else nc.vector
                 engine.tensor_tensor(t3[c - 1][:], part[c - 1][:], rs[c - 1][:], ALU.mult)
-        shift = sb([P, 2], F32, "shift")
-        nc.vector.tensor_scalar(shift[:], mass[:].bitcast(I32), -1.5 * LN2 / 2**23, 1.5 * LN2 * 127, ALU.mult, ALU.add)
-        low = [sb([P, 1], F32, f"low{c}")[:] for c in range(2)] + [shift[:, u : u + 1] for u in range(2)]
+        low = [sb([P, 1], F32, f"low{c}") for c in range(CHUNKS)]
         for c in range(CHUNKS):
             turn(neg[c][:], t3[c][:], False, True)
-            if c < 2:
-                nc.vector.tensor_reduce(low[c], neg[c][:], AX.X, ALU.min)
+            nc.vector.tensor_reduce(low[c][:], neg[c][:], AX.X, ALU.min)
         for c in range(CHUNKS):
-            nc.scalar.activation(prob[c][:], neg[c][:], ACT.Exp, bias=low[c], scale=-1.0, accum_out=tot[c][:])
+            nc.scalar.activation(prob[c][:], neg[c][:], ACT.Exp, bias=low[c][:], scale=-1.0, accum_out=tot[c][:])
         for c in range(CHUNKS + 1):
             if c < CHUNKS:
                 nc.vector.reciprocal(inv[c][:], tot[c][:])

@@ -278,6 +278,7 @@ def tile_picked_ystrip_soft_p_kernel(
             if c > 0:
                 u, n = divmod(c - 1, 2)
                 nc.vector.tensor_scalar(res[u][:, n, :], prob[c - 1][:], inv[c - 1][:], None, ALU.mult)
-                if n == 1:
-                    rows = out[u * HALF : (u + 1) * HALF, :]
-                    nc.sync.dma_start(rows.rearrange("(n p) v -> p n v", p=P), res[u][:])
+                if u == 1:
+                    nc.sync.dma_start(out[(c - 1) * P : c * P, :], res[u][:, n, :])
+                elif n == 1:
+                    nc.sync.dma_start(out[:HALF, :].rearrange("(n p) v -> p n v", p=P), res[u][:])

@@ -22,7 +22,7 @@ PACK = 4
 PASSES = K // (P * PACK)
 CHUNKS = S // P
 HALF = S // 2
-ES_ROW = 12
+ES_ROW = 4
 CAST_SPLIT = (64, 48)
 
 
@@ -126,8 +126,8 @@ def tile_picked_ystrip_soft_p_kernel(
         load_words(e_tab, e_words[0])
         cast_w(1)
         es_g = sb([P, S], U8, "es_g", tag="w_raw1")
-        nc.vector.memset(es_g[:].bitcast(I32), 0)
-        for r in range(4):
+        nc.vector.tensor_copy(es_g[:].bitcast(I32), es_c[:].bitcast(I32))
+        for r in range(1, 4):
             nc.sync.dma_start(es_g[ES_ROW + r : P : 32, :].bitcast(I32), es_c[4 + 8 * r : P : 32, :].bitcast(I32))
         quant_w(1)
         goal_sb = sb([P, CHUNKS, V], F32, "goal_sb", tag="w_bf1")

@@ -50,7 +50,7 @@ def tile_picked_ystrip_soft_p_kernel(
         xs_g = [sb([P, S], U8, "xs_g0")]
 
         nc.gpsimd.memset(es_tab[:].bitcast(I32), 0)
-        nc.gpsimd.memset(xs_tab[64:P, :].bitcast(I32), 0)
+        nc.vector.memset(xs_tab[64:P, :].bitcast(I32), 0)
         nc.gpsimd.memset(xs_tab[32:64, :].bitcast(I32), 0)
         nc.vector.memset(xs_g[0][:].bitcast(I32), 0)
 
@@ -173,7 +173,7 @@ def tile_picked_ystrip_soft_p_kernel(
             if c == 1:
                 nc.vector.tensor_copy(dst, src)
             else:
-                nc.scalar.activation(dst, src, ACT.Copy)
+                nc.scalar.copy(dst, src)
 
         def quant_h(c, codes):
             nc.vector.quantize_mx(codes.bitcast(FP8X4), hq_s[c][:], h_bf[c][:])

@@ -230,7 +230,7 @@ def tile_picked_ystrip_soft_p_kernel(
         for c in range(CHUNKS):
             turn(goal_ps[:, c, :], goal_sb[:, c, :], True, True)
         margin = sb([P, CHUNKS, P], F32, "margin")
-        nc.vector.tensor_scalar(margin[:], goal_ps[:], 0.9, None, ALU.mult)
+        nc.vector.tensor_scalar(margin[:], goal_ps[:], 0.3, None, ALU.mult)
 
         se_first = psum.tile([P, P], F32, name="se_first", tag="bank4")
         se_rest = psum.tile([P, CHUNKS - 1, P], F32, name="se_rest", tag="bank2")
@@ -259,19 +259,20 @@ def tile_picked_ystrip_soft_p_kernel(
         for c in range(1, CHUNKS + 1):
             if c < CHUNKS:
                 nc.vector.scalar_tensor_tensor(
-                    part[c][:], ses_ps[c // 2][:, c % 2, :], -3.0, rs[c][:], ALU.mult, ALU.mult
+                    part[c][:], ses_ps[c // 2][:, c % 2, :], -1.0, rs[c][:], ALU.mult, ALU.mult
                 )
             if c == 1:
-                nc.vector.scalar_tensor_tensor(t3[0][:], ses_ps[0][:, 0, :], -3.0, rs[0][:], ALU.mult, ALU.mult)
+                nc.vector.scalar_tensor_tensor(t3[0][:], ses_ps[0][:, 0, :], -1.0, rs[0][:], ALU.mult, ALU.mult)
             if c > 1:
                 engine = nc.gpsimd if c == 2 else nc.vector
                 engine.tensor_tensor(t3[c - 1][:], part[c - 1][:], rs[c - 1][:], ALU.mult)
+        logit = [sb([P, V], F32, f"logit{c}") for c in range(CHUNKS)]
         low = [sb([P, 1], F32, f"low{c}") for c in range(CHUNKS)]
         for c in range(CHUNKS):
             turn(neg[c][:], t3[c][:], False, True)
-            nc.vector.tensor_reduce(low[c][:], neg[c][:], AX.X, ALU.min)
+            nc.vector.tensor_scalar(logit[c][:], neg[c][:], 3.0, None, ALU.mult, ALU.min, accum_out=low[c][:])
         for c in range(CHUNKS):
-            nc.scalar.activation(prob[c][:], neg[c][:], ACT.Exp, bias=low[c][:], scale=-1.0, accum_out=tot[c][:])
+            nc.scalar.activation(prob[c][:], logit[c][:], ACT.Exp, bias=low[c][:], scale=-1.0, accum_out=tot[c][:])
         for c in range(CHUNKS + 1):
             if c < CHUNKS:
                 nc.vector.reciprocal(inv[c][:], tot[c][:])

from contextlib import ExitStack

import concourse.mybir as mybir
from concourse.masks import make_identity

K, T, S, H, D, V, W = 1024, 2048, 512, 512, 4, 128, 2048
FLOPS = 2 * K * H * S + 2 * H * S * D * V

F32 = mybir.dt.float32
BF16 = mybir.dt.bfloat16
I32 = mybir.dt.int32
U32 = mybir.dt.uint32
U16 = mybir.dt.uint16
U8 = mybir.dt.uint8
FP8X4 = mybir.dt.float8_e4m3fn_x4
ACT = mybir.ActivationFunctionType
ALU = mybir.AluOpType
AX = mybir.AxisListType

P = 128
PACK = 4
PASSES = K // (P * PACK)
CHUNKS = S // P
HALF = S // 2
ES_ROW = 4
CAST_SPLIT = (64, 48)


def tile_picked_ystrip_soft_p_kernel(
    tc, x_words, x_scales, w1, e_words, e_scales, goal, offs, cen, out
):
    nc = tc.nc
    with ExitStack() as ctx:
        keep = ctx.enter_context(tc.tile_pool(name="keep", bufs=1))
        psum = ctx.enter_context(tc.psum_pool(name="psum", bufs=1))

        def sb(shape, dtype, name, tag=None):
            return keep.tile(shape, dtype, name=name, tag=tag or name, align_bytes=64)

        def bank(n, name):
            return psum.tile([P, PACK, P], F32, name=name, tag=f"bank{n}")

        offs_sb = sb([P, S // 16], U16, "offs_sb")
        cen_sb = sb([P, S // 16], U16, "cen_sb")
        w_raw = [sb([P, PACK, H], F32, f"w_raw{g}") for g in range(PASSES)]
        xs_tab = sb([P, T], U8, "xs_tab")
        es_tab = sb([P, W], U8, "es_tab")
        xs_c = sb([P, S], U8, "xs_c")
        es_c = sb([P, S], U8, "es_c")
        xs_g = [sb([P, S], U8, "xs_g0")]

        nc.gpsimd.memset(es_tab[:].bitcast(I32), 0)
        nc.vector.memset(xs_tab[64:P, :].bitcast(I32), 0)
        nc.gpsimd.memset(xs_tab[32:64, :].bitcast(I32), 0)
        nc.vector.memset(xs_g[0][:].bitcast(I32), 0)

        def load_w(g):
            rows = w1[g * P * PACK : (g + 1) * P * PACK, :]
            nc.sync.dma_start(w_raw[g][:], rows.rearrange("(p j) c -> p j c", j=PACK))

        def load_words(tab, words):
            nc.sync.dma_start(tab[:], words.rearrange("p n r -> p (n r)").bitcast(I32))

        def place_x_scales(g):
            for r in range(4):
                nc.sync.dma_start(
                    xs_g[g][8 * g + r : P : 32, :].bitcast(I32),
                    xs_c[16 * g + r : 16 * g + 16 : 4, :].bitcast(I32),
                )

        nc.sync.dma_start(xs_tab[0:32, :].bitcast(I32), x_scales.rearrange("g q n -> (g q) n").bitcast(I32))
        nc.sync.dma_start(offs_sb[:], offs)
        load_w(0)
        nc.sync.dma_start(cen_sb[:], cen)
        nc.sync.dma_start(es_tab[4:P:8, :].bitcast(I32), e_scales[0].bitcast(I32))
        load_w(1)

        ident = sb([P, P], F32, "ident")
        make_identity(nc, ident[:])

        wq = [sb([P, H], U32, f"wq{g}") for g in range(PASSES)]
        wq_s = [sb([P, H], U8, f"wq_s{g}") for g in range(PASSES)]
        w_bf = [sb([P, H * PACK], BF16, f"w_bf{g}") for g in range(PASSES)]

        def cast_w(g):
            dst = w_bf[g][:].rearrange("p (t m j) -> p m t j", t=PACK, j=PACK)
            src = w_raw[g][:].rearrange("p j (m t) -> p m t j", t=PACK)
            split = CAST_SPLIT[g]
            nc.scalar.activation(dst[:, :split], src[:, :split], ACT.Copy)
            nc.vector.tensor_copy(dst[:, split:], src[:, split:])

        def quant_w(g):
            for u in range(2):
                cols = slice(u * H // 2, (u + 1) * H // 2)
                nc.vector.quantize_mx(
                    wq[g][:, cols].bitcast(FP8X4), wq_s[g][:, cols], w_bf[g][:, u * 2 * H : (u + 1) * 2 * H]
                )

        e_g = sb([P, S], U32, "e_g")
        x_width = (P, P)
        x_g = [[sb([P, n], U32, f"x_g{g}_{u}") for u in range(S // n)] for g, n in enumerate(x_width)]

        def gather_x(g):
            n = x_width[g]
            for u in range(S // n):
                cols = slice(u * n // 16, (u + 1) * n // 16)
                nc.vector.tensor_copy(x_g[g][u][:], x_tab[g][:].bitcast(U32).indirect(offs_sb[:, cols]))

        def x_codes(g, c):
            u, first = divmod(c * P, x_width[g])
            return x_g[g][u][:, first : first + P]

        nc.vector.tensor_copy(xs_c[:], xs_tab[:].indirect(offs_sb[:]))
        place_x_scales(0)
        x_tab = [sb([P, T], I32, "x_tab0", tag="xs_tab")]
        load_words(x_tab[0], x_words[0])
        cast_w(0)
        x_tab.append(sb([P, T], I32, "x_tab1", tag="w_raw0"))
        load_words(x_tab[1], x_words[1])
        nc.vector.tensor_copy(es_c[:], es_tab[:].indirect(cen_sb[:]))
        xs_g.append(sb([P, S], U8, "xs_g1", tag="es_tab"))
        nc.vector.memset(xs_g[1][:].bitcast(I32), 0)
        place_x_scales(1)
        quant_w(0)
        e_tab = sb([P, W], I32, "e_tab", tag="w_bf0")
        load_words(e_tab, e_words[0])
        cast_w(1)
        es_g = sb([P, S], U8, "es_g", tag="w_raw1")
        nc.vector.tensor_copy(es_g[:].bitcast(I32), es_c[:].bitcast(I32))
        for r in range(1, 4):
            nc.sync.dma_start(es_g[ES_ROW + r : P : 32, :].bitcast(I32), es_c[4 + 8 * r : P : 32, :].bitcast(I32))
        quant_w(1)
        goal_sb = sb([P, CHUNKS, V], F32, "goal_sb", tag="w_bf1")
        nc.sync.dma_start(goal_sb[:], goal.rearrange("(c p) v -> p c v", p=P))
        gather_x(0)
        gather_x(1)

        warm = psum.tile([P, H], F32, name="warm", tag="bank7")
        nc.tensor.matmul_mx(
            warm[:],
            lhsT=wq[1][:, :P].bitcast(FP8X4),
            lhsT_scale=wq_s[1][:, :P],
            rhs=wq[0][:].bitcast(FP8X4),
            rhs_scale=wq_s[0][:],
            start=True,
            stop=True,
        )

        h_ps = [bank(c, f"h_ps{c}") for c in range(CHUNKS)]
        def project(c, g, first, last):
            for j in range(PACK):
                nc.tensor.matmul_mx(
                    h_ps[c][:, j, :],
                    lhsT=wq[g][:, j * P : (j + 1) * P].bitcast(FP8X4),
                    lhsT_scale=wq_s[g][:, j * P : (j + 1) * P],
                    rhs=x_codes(g, c).bitcast(FP8X4),
                    rhs_scale=xs_g[g][8 * g : P, c * P : (c + 1) * P],
                    start=(first and j == 0),
                    stop=(last and j == PACK - 1),
                )

        for g in range(PASSES):
            for c in range(CHUNKS - 1):
                project(c, g, g == 0, g == PASSES - 1)
        for g in reversed(range(PASSES)):
            project(CHUNKS - 1, g, g == PASSES - 1, g == 0)

        h_bf = [sb([P, P * PACK], BF16, f"h_bf{c}") for c in range(CHUNKS)]
        hq_s = [sb([P, P], U8, f"hq_s{c}") for c in range(CHUNKS)]
        for c in range(CHUNKS):
            dst = h_bf[c][:].rearrange("p (t j) -> p t j", j=PACK)
            src = h_ps[c][:].rearrange("p j t -> p t j")
            if c == 1:
                nc.vector.tensor_copy(dst, src)
            else:
                nc.scalar.copy(dst, src)

        def quant_h(c, codes):
            nc.vector.quantize_mx(codes.bitcast(FP8X4), hq_s[c][:], h_bf[c][:])

        hq_early = sb([P, HALF], U32, "hq_early")
        hq = [hq_early[:, c * P : (c + 1) * P] for c in range(2)]
        for c in range(2):
            quant_h(c, hq[c])
        for u in range(4):
            cols = slice(u * P // 16, (u + 1) * P // 16)
            nc.vector.tensor_copy(e_g[:, u * P : (u + 1) * P], e_tab[:].bitcast(U32).indirect(cen_sb[:, cols]))
        hq_late = sb([P, HALF], U32, "hq_late", tag="es_c")
        hq.extend(hq_late[:, c * P : (c + 1) * P] for c in range(2))
        for c in range(2, CHUNKS):
            quant_h(c, hq[c])

        def turn(dst, src, start, stop):
            nc.tensor.matmul(dst, lhsT=src, rhs=ident[:], is_transpose=True, start=start, stop=stop)

        def sum_turned(dst, src):
            for d in range(D):
                turn(dst, src[:, d, :], d == 0, d == D - 1)

        ex_pair = [sb([P, 2, D, V], F32, f"ex{n}") for n in range(2)]
        es_pair = [sb([P, 2, D, V], F32, f"es{n}") for n in range(2)]
        ex = [ex_pair[c // 2][:, c % 2, :, :] for c in range(CHUNKS)]
        es = [es_pair[c // 2][:, c % 2, :, :] for c in range(CHUNKS)]

        def similarity(n, chunks, first, width):
            y_ps = psum.tile([P, len(chunks), width], F32, name=f"y_ps{n}", tag=f"bank{n}")
            for i, c in enumerate(chunks):
                nc.tensor.matmul_mx(
                    y_ps[:, i, :],
                    lhsT=hq[c].bitcast(FP8X4),
                    lhsT_scale=hq_s[c][:],
                    rhs=e_g[:, first : first + width].bitcast(FP8X4),
                    rhs_scale=es_g[ES_ROW:P, first : first + width],
                    start=True,
                    stop=True,
                )
            y_dv = y_ps[:].rearrange("p c (v d) -> p c d v", d=D)
            pair = slice(chunks[0] % 2, chunks[-1] % 2 + 1)
            classes = slice(first // D, (first + width) // D)
            ex_part = ex_pair[chunks[0] // 2][:, pair, :, classes]
            nc.scalar.activation(ex_part, y_dv, ACT.Exp, scale=2.0)
            nc.vector.tensor_tensor(es_pair[chunks[0] // 2][:, pair, :, classes], y_dv, ex_part, ALU.mult)

        for u in range(4):
            similarity((4, 5, 0, 1)[u], (0, 1), u * P, P)
        for c in range(2, CHUNKS):
            similarity(4 + c, (c,), 0, S)

        goal_ps = bank(3, "goal_ps")
        for c in range(CHUNKS):
            turn(goal_ps[:, c, :], goal_sb[:, c, :], True, True)
        margin = sb([P, CHUNKS, P], F32, "margin")
        nc.vector.tensor_scalar(margin[:], goal_ps[:], 0.3, None, ALU.mult)

        se_first = psum.tile([P, P], F32, name="se_first", tag="bank4")
        se_rest = psum.tile([P, CHUNKS - 1, P], F32, name="se_rest", tag="bank2")
        se_ps = [se_first[:]] + [se_rest[:, c, :] for c in range(CHUNKS - 1)]
        ses_ps = [psum.tile([P, 2, P], F32, name=f"ses_ps{u}", tag=f"bank{(5, 0)[u]}") for u in range(2)]
        for c in range(CHUNKS):
            sum_turned(se_ps[c], ex[c])
            if c > 0:
                sum_turned(ses_ps[(c - 1) // 2][:, (c - 1) % 2, :], es[c - 1])
        sum_turned(ses_ps[1][:, 1, :], es[CHUNKS - 1])

        rs_late = sb([P, 2, P], F32, "rs_late")
        rs = [sb([P, P], F32, f"rs{c}") for c in range(2)] + [rs_late[:, u, :] for u in range(2)]
        part = [sb([P, P], F32, f"part{c}") for c in range(CHUNKS)]
        t3 = [sb([P, P], F32, f"t3_{c}") for c in range(CHUNKS)]
        prob = [sb([P, V], F32, f"prob{c}") for c in range(CHUNKS)]
        tot = [sb([P, 1], F32, f"tot{c}") for c in range(CHUNKS)]
        inv = [sb([P, 1], F32, f"inv{c}") for c in range(CHUNKS)]
        res = [sb([P, 2, V], F32, f"res{u}") for u in range(2)]
        neg = [psum.tile([P, V], F32, name=f"neg{c}", tag=f"bank{(1, 6, 7, 3)[c]}") for c in range(CHUNKS)]
        for c in range(CHUNKS):
            turn(neg[c][:], margin[:, c, :], True, False)
        nc.vector.reciprocal(rs[0][:], se_ps[0])
        nc.scalar.activation(rs[1][:], se_ps[1], ACT.Abs_reciprocal_sqrt)
        nc.scalar.activation(rs_late[:], se_rest[:, 1:, :], ACT.Abs_reciprocal_sqrt)
        for c in range(1, CHUNKS + 1):
            if c < CHUNKS:
                nc.vector.scalar_tensor_tensor(
                    part[c][:], ses_ps[c // 2][:, c % 2, :], -1.0, rs[c][:], ALU.mult, ALU.mult
                )
            if c == 1:
                nc.vector.scalar_tensor_tensor(t3[0][:], ses_ps[0][:, 0, :], -1.0, rs[0][:], ALU.mult, ALU.mult)
            if c > 1:
                engine = nc.gpsimd if c == 2 else nc.vector
                engine.tensor_tensor(t3[c - 1][:], part[c - 1][:], rs[c - 1][:], ALU.mult)
        logit = [sb([P, V], F32, f"logit{c}") for c in range(CHUNKS)]
        low = [sb([P, 1], F32, f"low{c}") for c in range(CHUNKS)]
        for c in range(CHUNKS):
            turn(neg[c][:], t3[c][:], False, True)
            nc.vector.tensor_scalar(logit[c][:], neg[c][:], 3.0, None, ALU.mult, ALU.min, accum_out=low[c][:])
        for c in range(CHUNKS):
            nc.scalar.activation(prob[c][:], logit[c][:], ACT.Exp, bias=low[c][:], scale=-1.0, accum_out=tot[c][:])
        for c in range(CHUNKS + 1):
            if c < CHUNKS:
                nc.vector.reciprocal(inv[c][:], tot[c][:])
            if c > 0:
                u, n = divmod(c - 1, 2)
                nc.vector.tensor_scalar(res[u][:, n, :], prob[c - 1][:], inv[c - 1][:], None, ALU.mult)
                if u == 1:
                    nc.sync.dma_start(out[(c - 1) * P : c * P, :], res[u][:, n, :])
                elif n == 1:
                    nc.sync.dma_start(out[:HALF, :].rearrange("(n p) v -> p n v", p=P), res[u][:])
